import numpy as np
import ml_dtypes


def mxq(x, axis, fmt="e4m3"):
    dtype, down = {"e4m3": (ml_dtypes.float8_e4m3fn, 7), "e5m2": (ml_dtypes.float8_e5m2, 14)}[fmt]
    v = np.moveaxis(np.asarray(x, np.float32).astype(ml_dtypes.bfloat16).astype(np.float64), axis, -1)
    blocks = v.reshape(v.shape[:-1] + (-1, 32))
    amax = np.abs(blocks).max(-1, keepdims=True)
    byte = np.maximum(np.where(amax > 0, np.frexp(amax)[1] - 1 + 127, 0) - down, 1)
    scale = np.exp2(byte - 127.0)
    codes = (blocks / scale).astype(np.float32).astype(dtype).astype(np.float64)
    return np.moveaxis((codes * scale).reshape(v.shape), -1, axis)


WIDE = False


def mx_kscale(k):
    if not WIDE:
        return np.ones(k)
    levels = np.array([10, -10, 5, -5, 0])
    if k % 512:
        return np.exp2(np.random.permutation(np.resize(levels, k // 32))).repeat(32)
    a = np.empty((k // 512, 16))
    for p in range(k // 512):
        a[p, :8] = np.random.permutation(np.resize(levels, 8))
        for g in range(8):
            far = levels[np.abs(levels - a[p, g]) >= 10]
            a[p, g + 8] = far[np.random.randint(len(far))]
    return np.exp2(a.ravel()).repeat(32)


def f64(x):
    return np.asarray(x).astype(np.float64)


def striped(idx):
    return np.tile(idx.reshape(-1, 16).T, (8, 1)).astype(np.uint16)


def unstriped(offs):
    return offs[:16].T.reshape(-1).astype(np.int64)


def pack_weight(w):
    k, n = w.shape
    w = f64(np.asarray(w, np.float32).astype(ml_dtypes.bfloat16)).reshape(k // 32, 32, n)
    amax = np.abs(w).max(1)
    byte = np.clip(np.where(amax > 0, np.frexp(amax)[1] - 1 + 127 - 7, 1), 1, 254)
    scaled = (w * np.exp2(127.0 - byte)[:, None, :]).reshape(k, n).astype(np.float32)
    words = np.ascontiguousarray(scaled.reshape(k // 512, 128, 4, n).transpose(0, 1, 3, 2)).astype(ml_dtypes.float8_e4m3fn).view(np.uint8)
    return words, np.ascontiguousarray(byte.astype(np.uint8).reshape(k // 512, 16, n))


def unpack_weight(words, scales):
    g, p, n, _ = words.shape
    vals = np.ascontiguousarray(words).view(ml_dtypes.float8_e4m3fn).astype(np.float64) * np.repeat(np.exp2(scales.astype(np.float64) - 127.0), 8, axis=1)[..., None]
    return vals.transpose(0, 1, 3, 2).reshape(g * 512, n)


E2M1 = np.array([0.0, 0.5, 1.0, 1.5, 2.0, 3.0, 4.0, 6.0, -0.0, -0.5, -1.0, -1.5, -2.0, -3.0, -4.0, -6.0])


def pack_fp4(w):
    k, n = w.shape
    w = f64(np.asarray(w, np.float32).astype(ml_dtypes.bfloat16)).reshape(k // 32, 32, n)
    amax = np.abs(w).max(1)
    mant, ex = np.frexp(amax / 6.0)
    byte = np.clip(np.where(amax > 0, np.where(mant > 0.5, ex, ex - 1) + 127, 1), 1, 254)
    scaled = (w * np.exp2(127.0 - byte)[:, None, :]).reshape(k, n).astype(np.float32)
    c = np.ascontiguousarray(scaled.reshape(k // 512, 128, 4, n).transpose(0, 1, 3, 2)).astype(ml_dtypes.float4_e2m1fn).view(np.uint8) & 0xF
    words = (c[..., 0::2] | (c[..., 1::2] << 4)).reshape(k // 512, 128, 2 * n)
    return np.ascontiguousarray(words), np.ascontiguousarray(byte.astype(np.uint8).reshape(k // 512, 16, n))


def unpack_fp4(words, scales):
    g, _, n = scales.shape
    words = np.ascontiguousarray(words).reshape(g, 128, n, 2)
    nib = np.empty((g, 128, n, 4), np.uint8)
    nib[..., 0::2] = words & 0xF
    nib[..., 1::2] = words >> 4
    vals = E2M1[nib] * np.repeat(np.exp2(scales.astype(np.float64) - 127.0), 8, axis=1)[..., None]
    return vals.transpose(0, 1, 3, 2).reshape(g * 512, n)


def gelu(v):
    return 0.5 * v * (1.0 + np.tanh(np.sqrt(2.0 / np.pi) * (v + 0.044715 * v**3)))


K, T, S, H, N = 1024, 2048, 1024, 512, 128
P = 2 ** 7


def setup_inputs():
    n = np.random.standard_normal
    s = mx_kscale(K)[:, None]
    u = mx_kscale(H)
    packed_xT = pack_weight(n((K, T)) * s)
    packed_w2 = pack_fp4(n((H, N)) / np.sqrt(H) / u[:, None])
    return {
        "x_words": packed_xT[0],
        "x_scales": packed_xT[1],
        "w1": (n((K, H)) / np.sqrt(K) / s * u).astype(np.float32),
        "w2_words": packed_w2[0],
        "w2_scales": packed_w2[1],
        "share": np.tile(np.random.uniform(0.1, 0.9, S), (P, 1)).astype(np.float32),
        "offs": striped(np.random.permutation(T)[:S]),
        "par": striped(np.random.permutation(S)[(S * np.random.uniform(0, 1, S) ** 4).astype(np.int64)]),
    }


def reference(x_words, x_scales, w1, w2_words, w2_scales, share, offs, par):
    xq = unpack_weight(x_words, x_scales)[:, unstriped(offs)]
    h = gelu(mxq(f64(w1), 0, "e4m3").T @ xq)
    z = h + h[:, unstriped(par)] * f64(share)[:1]
    return unpack_fp4(w2_words, w2_scales).T @ mxq(z, 0, "e4m3")

@@ -1,0 +1,220 @@
+from contextlib import ExitStack
+
+import concourse.mybir as mybir
+from concourse.masks import make_identity
+
+K, T, S, H, N = 1024, 2048, 1024, 512, 128
+FLOPS = 2 * K * H * S + 2 * H * N * S
+
+F32 = mybir.dt.float32
+BF16 = mybir.dt.bfloat16
+I32 = mybir.dt.int32
+U32 = mybir.dt.uint32
+U16 = mybir.dt.uint16
+U8 = mybir.dt.uint8
+FP8X4 = mybir.dt.float8_e4m3fn_x4
+FP4X4 = mybir.dt.float4_e2m1fn_x4
+GELU = mybir.ActivationFunctionType.Gelu_apprx_tanh
+MULT = mybir.AluOpType.mult
+ADD = mybir.AluOpType.add
+
+P = 128
+PACK = 4
+PASSES = K // (P * PACK)
+BANK = 512
+HALVES = S // BANK
+LAST = 256
+
+
+def tile_picked_treeup_gelu_p_kernel(
+    tc, x_words, x_scales, w1, w2_words, w2_scales, share, offs, par, out
+):
+    nc = tc.nc
+    with ExitStack() as ctx:
+        keep = ctx.enter_context(tc.tile_pool(name="keep", bufs=1))
+        psum = ctx.enter_context(tc.psum_pool(name="psum", bufs=1))
+
+        def sb(name, shape, dtype, tag=None):
+            return keep.tile(shape, dtype, name=name, tag=tag or name, align_bytes=64)
+
+        def bank(name, b, shape):
+            return psum.tile(shape, F32, name=name, tag="bank%d" % b)
+
+        offs_sb = sb("offs_sb", [P, S // 16], U16)
+        par_sb = sb("par_sb", [P, S // 16], U16)
+        xw = [sb("xw%d" % g, [P, T], U32) for g in range(PASSES)]
+        xs = sb("xs", [P, T], U8)
+        w2s = sb("w2s", [P, N], U8)
+        w2w = sb("w2w", [P, 2 * N], U8)
+        share_sb = sb("share_sb", [P, S], F32)
+        raw = [[sb("raw%d_%d" % (g, c), [P, PACK, H // 2], F32) for c in range(2)] for g in range(PASSES)]
+        ident = sb("ident", [P, P], F32)
+        zero_in = sb("zero_in", [P, 1], F32)
+        zero_bias = sb("zero_bias", [P, 1], F32, tag="late")
+
+        nc.gpsimd.memset(xs[:].bitcast(I32), 0)
+        nc.gpsimd.memset(w2s[:].bitcast(I32), 0)
+        nc.gpsimd.memset(zero_in[:], 0.0)
+        make_identity(nc, ident[:])
+        nc.scalar.activation(zero_bias[:], zero_in[:], GELU)
+
+        def load_x(g):
+            nc.sync.dma_start(xw[g][:].bitcast(I32), x_words[g].rearrange("p n t -> p (n t)").bitcast(I32))
+
+        def load_w(g, c):
+            rows = w1[g * 512 : (g + 1) * 512, c * 256 : (c + 1) * 256]
+            nc.sync.dma_start(raw[g][c][:], rows.rearrange("(p j) c -> p j c", j=PACK))
+
+        nc.sync.dma_start(offs_sb[:], offs)
+        nc.sync.dma_start(par_sb[:], par)
+
+        for q in range(4):
+            nc.sync.dma_start(xs[32 * q : 32 * q + 8, :].bitcast(I32), x_scales[:, 4 * q : 4 * q + 4, :].bitcast(I32))
+        load_x(0)
+        load_w(0, 0)
+        load_w(0, 1)
+        load_x(1)
+        load_w(1, 0)
+        load_w(1, 1)
+        nc.sync.dma_start(share_sb[:], share)
+        nc.sync.dma_start(w2w[:].bitcast(I32), w2_words[0].bitcast(I32))
+        for q in range(4):
+            nc.sync.dma_start(w2s[32 * q : 32 * q + 4, :].bitcast(I32), w2_scales[0, 4 * q : 4 * q + 4, :].bitcast(I32))
+
+        gw = [sb("gw%d" % g, [P, S], U32) for g in range(PASSES)]
+        gs = sb("gs", [P, S], U8)
+        wb = [sb("wb%d" % g, [P, PACK, P, PACK], BF16) for g in range(PASSES)]
+        wq = [sb("wq%d" % g, [P, H], U32) for g in range(PASSES)]
+        wsc = [sb("wsc%d" % g, [P, H], U8) for g in range(PASSES)]
+
+        def cast(copy, g, c, m0, m1):
+            copy(
+                wb[g][:, :, 64 * c + m0 : 64 * c + m1, :].rearrange("p t m j -> p m t j"),
+                raw[g][c][:, :, PACK * m0 : PACK * m1].rearrange("p j (m t) -> p m t j", t=PACK),
+            )
+
+        def quantize_w(g, t0, t1):
+            nc.vector.quantize_mx(
+                out=wq[g][:, P * t0 : P * t1].bitcast(FP8X4),
+                scales=wsc[g][:, P * t0 : P * t1],
+                in_=wb[g][:, t0:t1, :, :].rearrange("p t m j -> p (t m j)"),
+            )
+
+        acc = [[bank("acc%d_%d" % (t, hf), HALVES * t + hf, [P, BANK]) for hf in range(HALVES)] for t in range(PACK)]
+
+        def layer1(g, t):
+            for hf in range(HALVES):
+                cols = slice(hf * BANK, (hf + 1) * BANK)
+                nc.tensor.matmul_mx(
+                    out=acc[t][hf][:],
+                    lhsT=wq[g][:, P * t : P * (t + 1)].bitcast(FP8X4),
+                    lhsT_scale=wsc[g][:, P * t : P * (t + 1)],
+                    rhs=gw[g][:, cols].bitcast(FP8X4),
+                    rhs_scale=gs[4 * g : P, cols],
+                    start=(g == 0),
+                    stop=(g == PASSES - 1),
+                )
+
+        nc.vector.tensor_copy(gs[:], xs[:].indirect(offs_sb[:]))
+        nc.vector.tensor_copy(gw[0][:], xw[0][:].indirect(offs_sb[:]))
+        cast(nc.scalar.copy, 0, 0, 0, 64)
+        cast(nc.scalar.copy, 0, 1, 0, 64)
+        quantize_w(0, 0, 4)
+        nc.vector.tensor_copy(gw[1][:], xw[1][:].indirect(offs_sb[:]))
+        cast(nc.scalar.copy, 1, 0, 0, 64)
+        cast(nc.scalar.copy, 1, 1, 0, 24)
+        cast(nc.vector.tensor_copy, 1, 1, 24, 64)
+        h = [sb("h%d" % t, [P, S], F32) for t in range(PACK)]
+        for t in range(PACK):
+            quantize_w(1, t, t + 1)
+            layer1(0, t)
+            layer1(1, t)
+            for hf in range(HALVES):
+                nc.scalar.activation(h[t][:, hf * BANK : (hf + 1) * BANK], acc[t][hf][:], GELU, bias=zero_bias[:])
+
+        early = sb("early", [P, PACK, BANK], F32)
+        late = sb("late", [P, PACK, S], F32, tag="late")
+        h_last = sb("h_last", [P, PACK, LAST], F32)
+        pieces = [(0, 512), (512, 768), (768, S)]
+        zq = {c0: sb("zq%d" % c0, [P, c1 - c0, PACK], BF16) for c0, c1 in pieces}
+
+        def zq_cols(c0, c1):
+            start = max(a for a, b in pieces if a <= c0)
+            return zq[start][:, c0 - start : c1 - start, :]
+
+        zc = sb("zc", [P, S], U32)
+        zs = sb("zs", [P, S], U8)
+        taken = {}
+
+        def follow(dst, t, c0, c1):
+            nc.vector.tensor_tensor(dst[:, t, c0:c1], h[t][:].indirect(par_sb[:, c0 // 16 : c1 // 16]), share_sb[:, c0:c1], MULT)
+            for b in range(c0 // P, c1 // P):
+                taken[(t, b)] = dst[:, t, b * P : (b + 1) * P]
+
+        zt = {}
+
+        def open_block(b, bk):
+            zt[b] = bank("zt%d" % b, bk, [P, PACK, P])
+            for t in range(PACK):
+                nc.tensor.matmul(zt[b][:, t, :], h[t][:, b * P : (b + 1) * P], ident[:], start=(t == 0), stop=False, is_transpose=True)
+
+        def close_blocks(blocks, bk):
+            nb = len(blocks)
+            rounded = [sb("rounded%d" % b, [P, 2, P, 2], BF16) for b in blocks]
+            back = bank("back%d" % blocks[0], bk, [P, nb, 2, P])
+            for i, b in enumerate(blocks):
+                for t in range(PACK):
+                    nc.tensor.matmul(zt[b][:, t, :], taken[(t, b)], ident[:], start=False, stop=(t == PACK - 1), is_transpose=True)
+                nc.scalar.copy(rounded[i][:], zt[b][:].rearrange("j (u e) p -> j u p e", e=2))
+            for i, b in enumerate(blocks):
+                for u in range(2):
+                    nc.tensor.transpose(back[:, i, u, :], rounded[i][:, u, :, :].rearrange("j p e -> j (p e)").bitcast(F32), ident[:])
+            c0, c1 = blocks[0] * P, (blocks[-1] + 1) * P
+            nc.scalar.copy(
+                zq_cols(c0, c1).rearrange("p j t -> p (j t)").bitcast(F32).rearrange("p (i j u) -> p i j u", i=nb, u=2),
+                back[:].rearrange("p i u j -> p i j u"),
+            )
+
+        def layer2(c0, c1, y, copy, tag=None):
+            nc.vector.quantize_mx(out=zc[:, c0:c1].bitcast(FP8X4), scales=zs[:, c0:c1], in_=zq_cols(c0, c1).rearrange("p j t -> p (j t)"))
+            nc.tensor.matmul_mx(out=y, lhsT=w2w[:].bitcast(FP4X4), lhsT_scale=w2s[:], rhs=zc[:, c0:c1].bitcast(FP8X4), rhs_scale=zs[:, c0:c1], start=True, stop=True)
+            res = sb("res%d" % c0, [P, c1 - c0], F32, tag=tag)
+            copy(res[:], y)
+            nc.sync.dma_start(out[:, c0:c1], res[:])
+
+        for b in range(4):
+            open_block(b, b)
+        follow(early, 0, 0, 512)
+        follow(early, 1, 0, 512)
+        follow(early, 2, 0, 256)
+        follow(early, 3, 0, 256)
+        close_blocks([0, 1], 4)
+        follow(late, 2, 256, 512)
+        follow(late, 3, 256, 512)
+        for b in (4, 5):
+            open_block(b, b + 2)
+        close_blocks([2, 3], 5)
+        for t in range(PACK):
+            nc.scalar.copy(h_last[:, t, :], h[t][:, S - LAST : S])
+        for t in range(PACK):
+            follow(late, t, 512, 768)
+        if LAST == 128:
+            open_block(6, 0)
+        close_blocks([4, 5], 4)
+        y_a = bank("y_a", 4, [P, BANK])
+        y_b = bank("y_b", 7, [P, BANK])
+        layer2(0, 512, y_a[:], nc.scalar.copy)
+        if LAST == 128:
+            for t in range(PACK):
+                follow(late, t, 768, 896)
+            close_blocks([6], 5)
+        for t in range(PACK):
+            follow(late, t, S - LAST, S)
+        layer2(512, 768, y_b[:, 0:256], nc.scalar.copy)
+        nc.vector.tensor_tensor(
+            zq_cols(S - LAST, S).rearrange("p (c i) t -> p c t i", i=4),
+            late[:, :, S - LAST : S].rearrange("p t (c i) -> p c t i", i=4),
+            h_last[:].rearrange("p t (c i) -> p c t i", i=4),
+            ADD,
+        )
+        layer2(768, S, y_b[:, 256:512], nc.scalar.copy)

@@ -47,22 +47,23 @@ def tile_picked_treeup_gelu_p_kernel(
         w2s = sb("w2s", [P, N], U8)
         w2w = sb("w2w", [P, 2 * N], U8)
         share_sb = sb("share_sb", [P, S], F32)
-        raw = [[sb("raw%d_%d" % (g, c), [P, PACK, H // 2], F32) for c in range(2)] for g in range(PASSES)]
+        widths = [[H], [H // 2, H // 2]]
+        raw = [[sb("raw%d_%d" % (g, c), [P, PACK, w], F32) for c, w in enumerate(widths[g])] for g in range(PASSES)]
         ident = sb("ident", [P, P], F32)
         zero_in = sb("zero_in", [P, 1], F32)
         zero_bias = sb("zero_bias", [P, 1], F32, tag="late")
 
         nc.gpsimd.memset(xs[:].bitcast(I32), 0)
-        nc.gpsimd.memset(w2s[:].bitcast(I32), 0)
-        nc.gpsimd.memset(zero_in[:], 0.0)
         make_identity(nc, ident[:])
+        nc.vector.memset(zero_in[:], 0.0)
+        nc.vector.memset(w2s[:].bitcast(I32), 0)
         nc.scalar.activation(zero_bias[:], zero_in[:], GELU)
 
         def load_x(g):
             nc.sync.dma_start(xw[g][:].bitcast(I32), x_words[g].rearrange("p n t -> p (n t)").bitcast(I32))
 
         def load_w(g, c):
-            rows = w1[g * 512 : (g + 1) * 512, c * 256 : (c + 1) * 256]
+            rows = w1[g * 512 : (g + 1) * 512, c * 256 : c * 256 + widths[g][c]]
             nc.sync.dma_start(raw[g][c][:], rows.rearrange("(p j) c -> p j c", j=PACK))
 
         nc.sync.dma_start(offs_sb[:], offs)
@@ -72,7 +73,6 @@ def tile_picked_treeup_gelu_p_kernel(
             nc.sync.dma_start(xs[32 * q : 32 * q + 8, :].bitcast(I32), x_scales[:, 4 * q : 4 * q + 4, :].bitcast(I32))
         load_x(0)
         load_w(0, 0)
-        load_w(0, 1)
         load_x(1)
         load_w(1, 0)
         load_w(1, 1)
@@ -117,13 +117,13 @@ def tile_picked_treeup_gelu_p_kernel(
 
         nc.vector.tensor_copy(gs[:], xs[:].indirect(offs_sb[:]))
         nc.vector.tensor_copy(gw[0][:], xw[0][:].indirect(offs_sb[:]))
-        cast(nc.scalar.copy, 0, 0, 0, 64)
-        cast(nc.scalar.copy, 0, 1, 0, 64)
+        cast(nc.scalar.copy, 0, 0, 0, 48)
+        cast(nc.vector.tensor_copy, 0, 0, 48, P)
         quantize_w(0, 0, 4)
         nc.vector.tensor_copy(gw[1][:], xw[1][:].indirect(offs_sb[:]))
         cast(nc.scalar.copy, 1, 0, 0, 64)
-        cast(nc.scalar.copy, 1, 1, 0, 24)
-        cast(nc.vector.tensor_copy, 1, 1, 24, 64)
+        cast(nc.scalar.copy, 1, 1, 0, 26)
+        cast(nc.vector.tensor_copy, 1, 1, 26, 64)
         h = [sb("h%d" % t, [P, S], F32) for t in range(PACK)]
         for t in range(PACK):
             quantize_w(1, t, t + 1)
@@ -135,38 +135,35 @@ def tile_picked_treeup_gelu_p_kernel(
         early = sb("early", [P, PACK, BANK], F32)
         late = sb("late", [P, PACK, S], F32, tag="late")
         h_last = sb("h_last", [P, PACK, LAST], F32)
-        pieces = [(0, 512), (512, 768), (768, S)]
+        pieces = [(0, 256), (256, 512), (512, 768), (768, S)]
         zq = {c0: sb("zq%d" % c0, [P, c1 - c0, PACK], BF16) for c0, c1 in pieces}
 
         def zq_cols(c0, c1):
             start = max(a for a, b in pieces if a <= c0)
             return zq[start][:, c0 - start : c1 - start, :]
 
-        zc = sb("zc", [P, S], U32)
         zs = sb("zs", [P, S], U8)
-        taken = {}
+        zt = {}
+
+        def turn_h(b, t):
+            nc.tensor.matmul(zt[b][:, t, :], h[t][:, b * P : (b + 1) * P], ident[:], start=(t == 0), stop=False, is_transpose=True)
 
         def follow(dst, t, c0, c1):
             nc.vector.tensor_tensor(dst[:, t, c0:c1], h[t][:].indirect(par_sb[:, c0 // 16 : c1 // 16]), share_sb[:, c0:c1], MULT)
+
+        def follow_and_turn(dst, t, c0, c1):
+            follow(dst, t, c0, c1)
             for b in range(c0 // P, c1 // P):
-                taken[(t, b)] = dst[:, t, b * P : (b + 1) * P]
+                if b < 4:
+                    turn_h(b, t)
+                nc.tensor.matmul(zt[b][:, t, :], dst[:, t, b * P : (b + 1) * P], ident[:], start=False, stop=(t == PACK - 1), is_transpose=True)
 
-        zt = {}
-
-        def open_block(b, bk):
-            zt[b] = bank("zt%d" % b, bk, [P, PACK, P])
-            for t in range(PACK):
-                nc.tensor.matmul(zt[b][:, t, :], h[t][:, b * P : (b + 1) * P], ident[:], start=(t == 0), stop=False, is_transpose=True)
-
-        def close_blocks(blocks, bk):
+        def turn_back(blocks, bk):
             nb = len(blocks)
             rounded = [sb("rounded%d" % b, [P, 2, P, 2], BF16) for b in blocks]
             back = bank("back%d" % blocks[0], bk, [P, nb, 2, P])
             for i, b in enumerate(blocks):
-                for t in range(PACK):
-                    nc.tensor.matmul(zt[b][:, t, :], taken[(t, b)], ident[:], start=False, stop=(t == PACK - 1), is_transpose=True)
                 nc.scalar.copy(rounded[i][:], zt[b][:].rearrange("j (u e) p -> j u p e", e=2))
-            for i, b in enumerate(blocks):
                 for u in range(2):
                     nc.tensor.transpose(back[:, i, u, :], rounded[i][:, u, :, :].rearrange("j p e -> j (p e)").bitcast(F32), ident[:])
             c0, c1 = blocks[0] * P, (blocks[-1] + 1) * P
@@ -175,46 +172,43 @@ def tile_picked_treeup_gelu_p_kernel(
                 back[:].rearrange("p i u j -> p i j u"),
             )
 
-        def layer2(c0, c1, y, copy, tag=None):
+        def layer2(c0, c1, bk, copy):
             nc.vector.quantize_mx(out=zc[:, c0:c1].bitcast(FP8X4), scales=zs[:, c0:c1], in_=zq_cols(c0, c1).rearrange("p j t -> p (j t)"))
-            nc.tensor.matmul_mx(out=y, lhsT=w2w[:].bitcast(FP4X4), lhsT_scale=w2s[:], rhs=zc[:, c0:c1].bitcast(FP8X4), rhs_scale=zs[:, c0:c1], start=True, stop=True)
-            res = sb("res%d" % c0, [P, c1 - c0], F32, tag=tag)
-            copy(res[:], y)
+            y = bank("y%d" % c0, bk, [P, c1 - c0])
+            nc.tensor.matmul_mx(out=y[:], lhsT=w2w[:].bitcast(FP4X4), lhsT_scale=w2s[:], rhs=zc[:, c0:c1].bitcast(FP8X4), rhs_scale=zs[:, c0:c1], start=True, stop=True)
+            res = sb("res%d" % c0, [P, c1 - c0], F32)
+            copy(res[:], y[:])
             nc.sync.dma_start(out[:, c0:c1], res[:])
 
         for b in range(4):
-            open_block(b, b)
-        follow(early, 0, 0, 512)
-        follow(early, 1, 0, 512)
-        follow(early, 2, 0, 256)
-        follow(early, 3, 0, 256)
-        close_blocks([0, 1], 4)
-        follow(late, 2, 256, 512)
-        follow(late, 3, 256, 512)
-        for b in (4, 5):
-            open_block(b, b + 2)
-        close_blocks([2, 3], 5)
+            zt[b] = bank("zt%d" % b, b, [P, PACK, P])
+        follow_and_turn(early, 0, 0, 512)
+        follow_and_turn(early, 1, 0, 512)
+        follow_and_turn(early, 2, 0, 256)
+        follow_and_turn(early, 3, 0, 256)
+        turn_back([0, 1], 4)
+        follow_and_turn(late, 2, 256, 512)
+        follow_and_turn(late, 3, 256, 512)
+        turn_back([2, 3], 5)
         for t in range(PACK):
             nc.scalar.copy(h_last[:, t, :], h[t][:, S - LAST : S])
-        for t in range(PACK):
-            follow(late, t, 512, 768)
-        if LAST == 128:
-            open_block(6, 0)
-        close_blocks([4, 5], 4)
-        y_a = bank("y_a", 4, [P, BANK])
-        y_b = bank("y_b", 7, [P, BANK])
-        layer2(0, 512, y_a[:], nc.scalar.copy)
-        if LAST == 128:
+        for b in (4, 5):
+            zt[b] = bank("zt%d" % b, b + 2, [P, PACK, P])
             for t in range(PACK):
-                follow(late, t, 768, 896)
-            close_blocks([6], 5)
+                turn_h(b, t)
+        for t in range(PACK):
+            follow_and_turn(late, t, 512, 768)
+        turn_back([4, 5], 4)
         for t in range(PACK):
             follow(late, t, S - LAST, S)
-        layer2(512, 768, y_b[:, 0:256], nc.scalar.copy)
         nc.vector.tensor_tensor(
             zq_cols(S - LAST, S).rearrange("p (c i) t -> p c t i", i=4),
             late[:, :, S - LAST : S].rearrange("p t (c i) -> p c t i", i=4),
             h_last[:].rearrange("p t (c i) -> p c t i", i=4),
             ADD,
         )
-        layer2(768, S, y_b[:, 256:512], nc.scalar.copy)
+        zc = sb("zc", [P, S], U32, tag="rounded5")
+        layer2(0, 256, 0, nc.scalar.copy)
+        layer2(256, 512, 1, nc.scalar.copy)
+        layer2(768, S, 2, nc.scalar.copy)
+        layer2(512, 768, 3, nc.vector.tensor_copy)

@@ -23,7 +23,7 @@ PACK = 4
 PASSES = K // (P * PACK)
 BANK = 512
 HALVES = S // BANK
-LAST = 256
+LAST = 384
 
 
 def tile_picked_treeup_gelu_p_kernel(
@@ -132,83 +132,110 @@ def tile_picked_treeup_gelu_p_kernel(
             for hf in range(HALVES):
                 nc.scalar.activation(h[t][:, hf * BANK : (hf + 1) * BANK], acc[t][hf][:], GELU, bias=zero_bias[:])
 
-        early = sb("early", [P, PACK, BANK], F32)
-        late = sb("late", [P, PACK, S], F32, tag="late")
+        TURNED = S - LAST
+        groups = [list(range(b, min(b + 2, TURNED // P))) for b in range(0, TURNED // P, 2)]
         h_last = sb("h_last", [P, PACK, LAST], F32)
-        pieces = [(0, 256), (256, 512), (512, 768), (768, S)]
-        zq = {c0: sb("zq%d" % c0, [P, c1 - c0, PACK], BF16) for c0, c1 in pieces}
+
+        taken = {}
+
+        def follow(dst, t, c0, c1):
+            nc.vector.tensor_tensor(dst, h[t][:].indirect(par_sb[:, c0 // 16 : c1 // 16]), share_sb[:, c0:c1], MULT)
+            for b in range(c0 // P, c1 // P):
+                taken[t, b] = dst[:, b * P - c0 : (b + 1) * P - c0]
+
+        sums = {}
+        rounded = {(u, i): sb("rounded%d_%d" % (u, i), [P, 2, P, 2], BF16) for u in range(2) for i in range(len(groups))}
+
+        def turn_h(t, i):
+            u, e = divmod(t, 2)
+            if e == 0:
+                sums[u, i] = bank("sum%d_%d" % (u, i), 4 * u + i, [P, 2, 2, P])
+            for n, b in enumerate(groups[i]):
+                nc.tensor.matmul(sums[u, i][:, n, e, :], h[t][:, b * P : (b + 1) * P], ident[:], start=(e == 0 and n == 0), stop=False, is_transpose=True)
+
+        def turn_taken(t, i):
+            u, e = divmod(t, 2)
+            for n, b in enumerate(groups[i]):
+                nc.tensor.matmul(sums[u, i][:, n, e, :], taken[t, b], ident[:], start=False, stop=(e == 1 and b == groups[i][-1]), is_transpose=True)
+
+        def round_sums(u, i):
+            nb = len(groups[i])
+            nc.scalar.copy(rounded[u, i][:, 0:nb, :, :], sums[u, i][:, 0:nb, :, :].rearrange("j n e p -> j n p e"))
+
+        pieces = [(0, 512), (512, 768), (768, S)]
+        zq = {c0: sb("zq%d" % c0, [P, c1 - c0, PACK], BF16) for c0, c1 in pieces[:2]}
 
         def zq_cols(c0, c1):
             start = max(a for a, b in pieces if a <= c0)
             return zq[start][:, c0 - start : c1 - start, :]
 
-        zs = sb("zs", [P, S], U8)
-        zt = {}
+        backs = {}
 
-        def turn_h(b, t):
-            nc.tensor.matmul(zt[b][:, t, :], h[t][:, b * P : (b + 1) * P], ident[:], start=(t == 0), stop=False, is_transpose=True)
+        def turn_back(u, i):
+            if u == 0:
+                backs[i] = bank("back%d" % i, i, [P, 2, 2, P])
+            for n in range(len(groups[i])):
+                nc.tensor.transpose(backs[i][:, n, u, :], rounded[u, i][:, n, :, :].rearrange("j p e -> j (p e)").bitcast(F32), ident[:])
 
-        def follow(dst, t, c0, c1):
-            nc.vector.tensor_tensor(dst[:, t, c0:c1], h[t][:].indirect(par_sb[:, c0 // 16 : c1 // 16]), share_sb[:, c0:c1], MULT)
-
-        def follow_and_turn(dst, t, c0, c1):
-            follow(dst, t, c0, c1)
-            for b in range(c0 // P, c1 // P):
-                if b < 4:
-                    turn_h(b, t)
-                nc.tensor.matmul(zt[b][:, t, :], dst[:, t, b * P : (b + 1) * P], ident[:], start=False, stop=(t == PACK - 1), is_transpose=True)
-
-        def turn_back(blocks, bk):
-            nb = len(blocks)
-            rounded = [sb("rounded%d" % b, [P, 2, P, 2], BF16) for b in blocks]
-            back = bank("back%d" % blocks[0], bk, [P, nb, 2, P])
-            for i, b in enumerate(blocks):
-                nc.scalar.copy(rounded[i][:], zt[b][:].rearrange("j (u e) p -> j u p e", e=2))
-                for u in range(2):
-                    nc.tensor.transpose(back[:, i, u, :], rounded[i][:, u, :, :].rearrange("j p e -> j (p e)").bitcast(F32), ident[:])
-            c0, c1 = blocks[0] * P, (blocks[-1] + 1) * P
+        def weave(i):
+            nb = len(groups[i])
+            c0 = groups[i][0] * P
             nc.scalar.copy(
-                zq_cols(c0, c1).rearrange("p j t -> p (j t)").bitcast(F32).rearrange("p (i j u) -> p i j u", i=nb, u=2),
-                back[:].rearrange("p i u j -> p i j u"),
+                zq_cols(c0, c0 + nb * P).rearrange("p j t -> p (j t)").bitcast(F32).rearrange("p (n j u) -> p n j u", n=nb, u=2),
+                backs[i][:, 0:nb, :, :].rearrange("p n u j -> p n j u"),
             )
 
-        def layer2(c0, c1, bk, copy):
+        zc = sb("zc", [P, S], U32)
+        zs = sb("zs", [P, S], U8)
+
+        def quantize_z(c0, c1):
             nc.vector.quantize_mx(out=zc[:, c0:c1].bitcast(FP8X4), scales=zs[:, c0:c1], in_=zq_cols(c0, c1).rearrange("p j t -> p (j t)"))
+
+        def layer2(c0, c1, bk, copy):
             y = bank("y%d" % c0, bk, [P, c1 - c0])
             nc.tensor.matmul_mx(out=y[:], lhsT=w2w[:].bitcast(FP4X4), lhsT_scale=w2s[:], rhs=zc[:, c0:c1].bitcast(FP8X4), rhs_scale=zs[:, c0:c1], start=True, stop=True)
             res = sb("res%d" % c0, [P, c1 - c0], F32)
             copy(res[:], y[:])
             nc.sync.dma_start(out[:, c0:c1], res[:])
 
-        for b in range(4):
-            zt[b] = bank("zt%d" % b, b, [P, PACK, P])
-        follow_and_turn(early, 0, 0, 512)
-        follow_and_turn(early, 1, 0, 512)
-        follow_and_turn(early, 2, 0, 256)
-        follow_and_turn(early, 3, 0, 256)
-        turn_back([0, 1], 4)
-        follow_and_turn(late, 2, 256, 512)
-        follow_and_turn(late, 3, 256, 512)
-        turn_back([2, 3], 5)
+        early = sb("early", [P, PACK, TURNED], F32)
+        every = range(len(groups))
+        for u in range(2):
+            for t in (2 * u, 2 * u + 1):
+                for i in every:
+                    turn_h(t, i)
+            follow(early[:, 2 * u, :], 2 * u, 0, TURNED)
+            for i in every:
+                turn_taken(2 * u, i)
+            for i in every:
+                c0, c1 = groups[i][0] * P, (groups[i][-1] + 1) * P
+                follow(early[:, 2 * u + 1, c0:c1], 2 * u + 1, c0, c1)
+                turn_taken(2 * u + 1, i)
+                round_sums(u, i)
+            for i in every:
+                turn_back(u, i)
+        for i in every:
+            weave(i)
         for t in range(PACK):
-            nc.scalar.copy(h_last[:, t, :], h[t][:, S - LAST : S])
-        for b in (4, 5):
-            zt[b] = bank("zt%d" % b, b + 2, [P, PACK, P])
-            for t in range(PACK):
-                turn_h(b, t)
+            nc.sync.dma_start(h_last[:, t, :], h[t][:, TURNED:S])
+        last = sb("last", [P, PACK, LAST], F32, tag="late")
         for t in range(PACK):
-            follow_and_turn(late, t, 512, 768)
-        turn_back([4, 5], 4)
-        for t in range(PACK):
-            follow(late, t, S - LAST, S)
-        nc.vector.tensor_tensor(
-            zq_cols(S - LAST, S).rearrange("p (c i) t -> p c t i", i=4),
-            late[:, :, S - LAST : S].rearrange("p t (c i) -> p c t i", i=4),
-            h_last[:].rearrange("p t (c i) -> p c t i", i=4),
-            ADD,
-        )
-        zc = sb("zc", [P, S], U32, tag="rounded5")
-        layer2(0, 256, 0, nc.scalar.copy)
-        layer2(256, 512, 1, nc.scalar.copy)
-        layer2(768, S, 2, nc.scalar.copy)
-        layer2(512, 768, 3, nc.vector.tensor_copy)
+            follow(last[:, t, :], t, TURNED, S)
+
+        def add(c0, c1):
+            nc.vector.tensor_tensor(
+                zq_cols(c0, c1).rearrange("p (c i) t -> p c t i", i=4),
+                last[:, :, c0 - TURNED : c1 - TURNED].rearrange("p t (c i) -> p c t i", i=4),
+                h_last[:, :, c0 - TURNED : c1 - TURNED].rearrange("p t (c i) -> p c t i", i=4),
+                ADD,
+            )
+
+        quantize_z(0, BANK)
+        layer2(0, BANK, len(groups) - 1, nc.scalar.copy)
+        add(TURNED, 768)
+        zq[768] = sb("zq768", [P, 256, PACK], BF16, tag="zq0")
+        add(768, S)
+        quantize_z(BANK, 768)
+        layer2(BANK, 768, 5, nc.scalar.copy)
+        quantize_z(768, S)
+        layer2(768, S, 6, nc.vector.tensor_copy)

@@ -44,45 +44,50 @@ def tile_picked_treeup_gelu_p_kernel(
         par_sb = sb("par_sb", [P, S // 16], U16)
         xw = [sb("xw%d" % g, [P, T], U32) for g in range(PASSES)]
         xs = sb("xs", [P, T], U8)
-        w2s = sb("w2s", [P, N], U8)
-        w2w = sb("w2w", [P, 2 * N], U8)
-        share_sb = sb("share_sb", [P, S], F32)
-        widths = [[H], [H // 2, H // 2]]
-        raw = [[sb("raw%d_%d" % (g, c), [P, PACK, w], F32) for c, w in enumerate(widths[g])] for g in range(PASSES)]
+        raw0 = sb("raw0", [P, PACK, H], F32)
+        plane0 = sb("plane0", [P, S], U8)
         ident = sb("ident", [P, P], F32)
         zero_in = sb("zero_in", [P, 1], F32)
         zero_bias = sb("zero_bias", [P, 1], F32, tag="late")
 
-        nc.gpsimd.memset(xs[:].bitcast(I32), 0)
+        nc.gpsimd.memset(xs[32:64, :].bitcast(I32), 0)
+        nc.gpsimd.memset(xs[64:P, :].bitcast(I32), 0)
+        nc.gpsimd.memset(plane0[:].bitcast(I32), 0)
         make_identity(nc, ident[:])
         nc.vector.memset(zero_in[:], 0.0)
-        nc.vector.memset(w2s[:].bitcast(I32), 0)
         nc.scalar.activation(zero_bias[:], zero_in[:], GELU)
 
         def load_x(g):
             nc.sync.dma_start(xw[g][:].bitcast(I32), x_words[g].rearrange("p n t -> p (n t)").bitcast(I32))
 
-        def load_w(g, c):
-            rows = w1[g * 512 : (g + 1) * 512, c * 256 : c * 256 + widths[g][c]]
-            nc.sync.dma_start(raw[g][c][:], rows.rearrange("(p j) c -> p j c", j=PACK))
+        def w_rows(g, c0, c1):
+            return w1[g * 512 : (g + 1) * 512, c0:c1].rearrange("(p j) c -> p j c", j=PACK)
 
         nc.sync.dma_start(offs_sb[:], offs)
-        nc.sync.dma_start(par_sb[:], par)
-
-        for q in range(4):
-            nc.sync.dma_start(xs[32 * q : 32 * q + 8, :].bitcast(I32), x_scales[:, 4 * q : 4 * q + 4, :].bitcast(I32))
+        nc.sync.dma_start(xs[0:32, :].bitcast(I32), x_scales.rearrange("g q n -> (g q) n").bitcast(I32))
         load_x(0)
-        load_w(0, 0)
+        nc.sync.dma_start(raw0[:], w_rows(0, 0, H))
         load_x(1)
-        load_w(1, 0)
-        load_w(1, 1)
-        nc.sync.dma_start(share_sb[:], share)
-        nc.sync.dma_start(w2w[:].bitcast(I32), w2_words[0].bitcast(I32))
-        for q in range(4):
-            nc.sync.dma_start(w2s[32 * q : 32 * q + 4, :].bitcast(I32), w2_scales[0, 4 * q : 4 * q + 4, :].bitcast(I32))
+        nc.sync.dma_start(par_sb[:], par)
 
         gw = [sb("gw%d" % g, [P, S], U32) for g in range(PASSES)]
         gs = sb("gs", [P, S], U8)
+
+        def place_scales(queue, plane, g):
+            for q in range(4):
+                queue.dma_start(plane[32 * q : 32 * q + 4, :].bitcast(I32), gs[16 * g + 4 * q : 16 * g + 4 * q + 4, :].bitcast(I32))
+
+        nc.vector.tensor_copy(gs[:], xs[:].indirect(offs_sb[:]))
+        place_scales(nc.scalar, plane0, 0)
+        raw1 = sb("raw1", [P, 2, PACK, H // 2], F32, tag="xs")
+        for c in range(2):
+            nc.sync.dma_start(raw1[:, c, :, :], w_rows(1, c * 256, (c + 1) * 256))
+        raw = [[raw0[:]], [raw1[:, 0, :, :], raw1[:, 1, :, :]]]
+        nc.vector.tensor_copy(gw[0][:], xw[0][:].indirect(offs_sb[:]))
+        plane1 = sb("plane1", [P, S], U8, tag="xw0")
+        nc.gpsimd.memset(plane1[:].bitcast(I32), 0)
+        place_scales(nc.sync, plane1, 1)
+        planes = [plane0, plane1]
         wb = [sb("wb%d" % g, [P, PACK, P, PACK], BF16) for g in range(PASSES)]
         wq = [sb("wq%d" % g, [P, H], U32) for g in range(PASSES)]
         wsc = [sb("wsc%d" % g, [P, H], U8) for g in range(PASSES)]
@@ -110,17 +115,23 @@ def tile_picked_treeup_gelu_p_kernel(
                     lhsT=wq[g][:, P * t : P * (t + 1)].bitcast(FP8X4),
                     lhsT_scale=wsc[g][:, P * t : P * (t + 1)],
                     rhs=gw[g][:, cols].bitcast(FP8X4),
-                    rhs_scale=gs[4 * g : P, cols],
+                    rhs_scale=planes[g][:, cols],
                     start=(g == 0),
                     stop=(g == PASSES - 1),
                 )
 
-        nc.vector.tensor_copy(gs[:], xs[:].indirect(offs_sb[:]))
-        nc.vector.tensor_copy(gw[0][:], xw[0][:].indirect(offs_sb[:]))
-        cast(nc.scalar.copy, 0, 0, 0, 48)
-        cast(nc.vector.tensor_copy, 0, 0, 48, P)
+        cast(nc.scalar.copy, 0, 0, 0, 64)
+        cast(nc.vector.tensor_copy, 0, 0, 64, P)
         quantize_w(0, 0, 4)
+        share_sb = sb("share_sb", [P, S], F32, tag="raw0")
+        nc.sync.dma_start(share_sb[:], share)
+        w2w = sb("w2w", [P, 2 * N], U8, tag="wb0")
+        nc.sync.dma_start(w2w[:].bitcast(I32), w2_words[0].bitcast(I32))
         nc.vector.tensor_copy(gw[1][:], xw[1][:].indirect(offs_sb[:]))
+        w2s = sb("w2s", [P, N], U8, tag="xw1")
+        nc.gpsimd.memset(w2s[:].bitcast(I32), 0)
+        for q in range(4):
+            nc.sync.dma_start(w2s[32 * q : 32 * q + 4, :].bitcast(I32), w2_scales[0, 4 * q : 4 * q + 4, :].bitcast(I32))
         cast(nc.scalar.copy, 1, 0, 0, 64)
         cast(nc.scalar.copy, 1, 1, 0, 26)
         cast(nc.vector.tensor_copy, 1, 1, 26, 64)
@@ -207,9 +218,12 @@ def tile_picked_treeup_gelu_p_kernel(
             follow(early[:, 2 * u, :], 2 * u, 0, TURNED)
             for i in every:
                 turn_taken(2 * u, i)
+            if u == 0:
+                follow(early[:, 1, :], 1, 0, TURNED)
             for i in every:
                 c0, c1 = groups[i][0] * P, (groups[i][-1] + 1) * P
-                follow(early[:, 2 * u + 1, c0:c1], 2 * u + 1, c0, c1)
+                if u == 1:
+                    follow(early[:, 3, c0:c1], 3, c0, c1)
                 turn_taken(2 * u + 1, i)
                 round_sums(u, i)
             for i in every:

@@ -24,6 +24,9 @@ PASSES = K // (P * PACK)
 BANK = 512
 HALVES = S // BANK
 LAST = 384
+ROW0 = 12
+SUM_BANKS = ((6, 7, 2), (4, 5, 3))
+PLANE_START = (12, 0)
 
 
 def tile_picked_treeup_gelu_p_kernel(
@@ -44,70 +47,79 @@ def tile_picked_treeup_gelu_p_kernel(
         par_sb = sb("par_sb", [P, S // 16], U16)
         xw = [sb("xw%d" % g, [P, T], U32) for g in range(PASSES)]
         xs = sb("xs", [P, T], U8)
-        raw0 = sb("raw0", [P, PACK, H], F32)
-        plane0 = sb("plane0", [P, S], U8)
+        raw = [sb("raw0", [P, PACK, H], F32)]
         ident = sb("ident", [P, P], F32)
         zero_in = sb("zero_in", [P, 1], F32)
         zero_bias = sb("zero_bias", [P, 1], F32, tag="late")
 
         nc.gpsimd.memset(xs[32:64, :].bitcast(I32), 0)
+        nc.gpsimd.memset(xs[0:ROW0, :].bitcast(I32), 0)
         nc.gpsimd.memset(xs[64:P, :].bitcast(I32), 0)
-        nc.gpsimd.memset(plane0[:].bitcast(I32), 0)
         make_identity(nc, ident[:])
         nc.vector.memset(zero_in[:], 0.0)
         nc.scalar.activation(zero_bias[:], zero_in[:], GELU)
 
-        def load_x(g):
-            nc.sync.dma_start(xw[g][:].bitcast(I32), x_words[g].rearrange("p n t -> p (n t)").bitcast(I32))
-
-        def w_rows(g, c0, c1):
-            return w1[g * 512 : (g + 1) * 512, c0:c1].rearrange("(p j) c -> p j c", j=PACK)
-
         nc.sync.dma_start(offs_sb[:], offs)
-        nc.sync.dma_start(xs[0:32, :].bitcast(I32), x_scales.rearrange("g q n -> (g q) n").bitcast(I32))
-        load_x(0)
-        nc.sync.dma_start(raw0[:], w_rows(0, 0, H))
-        load_x(1)
         nc.sync.dma_start(par_sb[:], par)
+
+        def load_x(g, c0, c1):
+            nc.sync.dma_start(xw[g][:, c0:c1].bitcast(I32), x_words[g][:, c0:c1, :].rearrange("p n t -> p (n t)").bitcast(I32))
+
+        def load_w(g):
+            nc.sync.dma_start(raw[g][:], w1[g * 512 : (g + 1) * 512, :].rearrange("(p j) c -> p j c", j=PACK))
+
+        share_col = sb("share_col", [P, S // P], F32)
+        nc.sync.dma_start(share_col[:], share[0:1, :].rearrange("o (p c) -> (o p) c", p=P))
+        load_x(0, 0, T // 4)
+        nc.sync.dma_start(xs[ROW0 : ROW0 + 32, :].bitcast(I32), x_scales.rearrange("g q n -> (g q) n").bitcast(I32))
+        load_x(0, T // 4, T)
+        load_w(0)
+        load_x(1, 0, T)
+
+        share_sb = sb("share_sb", [P, S], F32)
+        for hf in range(HALVES):
+            spread = bank("spread%d" % hf, hf, [P, PACK, P])
+            for c in range(PACK):
+                nc.tensor.transpose(spread[:, c, :], share_col[:, PACK * hf + c : PACK * hf + c + 1].to_broadcast([P, P]), ident[:])
+            nc.scalar.copy(
+                share_sb[:].rearrange("p (j c) -> p j c", c=S // P)[:, :, PACK * hf : PACK * (hf + 1)],
+                spread[:].rearrange("p c j -> p j c"),
+            )
 
         gw = [sb("gw%d" % g, [P, S], U32) for g in range(PASSES)]
         gs = sb("gs", [P, S], U8)
-
-        def place_scales(queue, plane, g):
-            for q in range(4):
-                queue.dma_start(plane[32 * q : 32 * q + 4, :].bitcast(I32), gs[16 * g + 4 * q : 16 * g + 4 * q + 4, :].bitcast(I32))
-
+        planes = sb("planes", [P, S], U8)
         nc.vector.tensor_copy(gs[:], xs[:].indirect(offs_sb[:]))
-        place_scales(nc.scalar, plane0, 0)
-        raw1 = sb("raw1", [P, 2, PACK, H // 2], F32, tag="xs")
-        for c in range(2):
-            nc.sync.dma_start(raw1[:, c, :, :], w_rows(1, c * 256, (c + 1) * 256))
-        raw = [[raw0[:]], [raw1[:, 0, :, :], raw1[:, 1, :, :]]]
+        nc.vector.tensor_copy(planes[:].bitcast(I32), gs[:].bitcast(I32))
+        for g in range(PASSES):
+            for q in range(4):
+                source, target = ROW0 + 16 * g + 4 * q, 32 * q + PLANE_START[g]
+                if source != target:
+                    nc.scalar.dma_start(planes[target : target + 4, :].bitcast(I32), gs[source : source + 4, :].bitcast(I32))
+        raw.append(sb("raw1", [P, PACK, H], F32, tag="xs"))
+        load_w(1)
         nc.vector.tensor_copy(gw[0][:], xw[0][:].indirect(offs_sb[:]))
-        plane1 = sb("plane1", [P, S], U8, tag="xw0")
-        nc.gpsimd.memset(plane1[:].bitcast(I32), 0)
-        place_scales(nc.sync, plane1, 1)
-        planes = [plane0, plane1]
-        wb = [sb("wb%d" % g, [P, PACK, P, PACK], BF16) for g in range(PASSES)]
         wq = [sb("wq%d" % g, [P, H], U32) for g in range(PASSES)]
         wsc = [sb("wsc%d" % g, [P, H], U8) for g in range(PASSES)]
 
-        def cast(copy, g, c, m0, m1):
+        def cast(copy, wb, g, t0, t1, m0, m1):
             copy(
-                wb[g][:, :, 64 * c + m0 : 64 * c + m1, :].rearrange("p t m j -> p m t j"),
-                raw[g][c][:, :, PACK * m0 : PACK * m1].rearrange("p j (m t) -> p m t j", t=PACK),
+                wb[:, :, m0:m1, :].rearrange("p t m j -> p m t j"),
+                raw[g][:, :, PACK * m0 : PACK * m1].rearrange("p j (m t) -> p m t j", t=PACK)[:, :, t0:t1, :],
             )
 
-        def quantize_w(g, t0, t1):
+        def quantize_w(wb, g, t0, t1):
             nc.vector.quantize_mx(
                 out=wq[g][:, P * t0 : P * t1].bitcast(FP8X4),
                 scales=wsc[g][:, P * t0 : P * t1],
-                in_=wb[g][:, t0:t1, :, :].rearrange("p t m j -> p (t m j)"),
+                in_=wb[:].rearrange("p t m j -> p (t m j)"),
             )
 
-        acc = [[bank("acc%d_%d" % (t, hf), HALVES * t + hf, [P, BANK]) for hf in range(HALVES)] for t in range(PACK)]
+        acc = {}
 
         def layer1(g, t):
+            if g == 0:
+                acc[t] = [bank("acc%d_%d" % (t, hf), HALVES * (t % 3) + hf, [P, BANK]) for hf in range(HALVES)]
             for hf in range(HALVES):
                 cols = slice(hf * BANK, (hf + 1) * BANK)
                 nc.tensor.matmul_mx(
@@ -115,16 +127,17 @@ def tile_picked_treeup_gelu_p_kernel(
                     lhsT=wq[g][:, P * t : P * (t + 1)].bitcast(FP8X4),
                     lhsT_scale=wsc[g][:, P * t : P * (t + 1)],
                     rhs=gw[g][:, cols].bitcast(FP8X4),
-                    rhs_scale=planes[g][:, cols],
+                    rhs_scale=planes[PLANE_START[g] : P, cols],
                     start=(g == 0),
                     stop=(g == PASSES - 1),
                 )
 
-        cast(nc.scalar.copy, 0, 0, 0, 64)
-        cast(nc.vector.tensor_copy, 0, 0, 64, P)
-        quantize_w(0, 0, 4)
-        share_sb = sb("share_sb", [P, S], F32, tag="raw0")
-        nc.sync.dma_start(share_sb[:], share)
+        wb0 = sb("wb0", [P, PACK, P, PACK], BF16)
+        cast(nc.scalar.copy, wb0, 0, 0, PACK, 0, 80)
+        cast(nc.vector.tensor_copy, wb0, 0, 0, PACK, 80, P)
+        quantize_w(wb0, 0, 0, PACK)
+        for t in range(PACK - 1):
+            layer1(0, t)
         w2w = sb("w2w", [P, 2 * N], U8, tag="wb0")
         nc.sync.dma_start(w2w[:].bitcast(I32), w2_words[0].bitcast(I32))
         nc.vector.tensor_copy(gw[1][:], xw[1][:].indirect(offs_sb[:]))
@@ -132,13 +145,21 @@ def tile_picked_treeup_gelu_p_kernel(
         nc.gpsimd.memset(w2s[:].bitcast(I32), 0)
         for q in range(4):
             nc.sync.dma_start(w2s[32 * q : 32 * q + 4, :].bitcast(I32), w2_scales[0, 4 * q : 4 * q + 4, :].bitcast(I32))
-        cast(nc.scalar.copy, 1, 0, 0, 64)
-        cast(nc.scalar.copy, 1, 1, 0, 26)
-        cast(nc.vector.tensor_copy, 1, 1, 26, 64)
+        first = sb("first", [P, 1, P, PACK], BF16, tag="wb1")
+        cast(nc.scalar.copy, first, 1, 0, 1, 0, 48)
+        cast(nc.vector.tensor_copy, first, 1, 0, 1, 48, P)
+        quantize_w(first, 1, 0, 1)
+        second = sb("second", [P, 1, P, PACK], BF16)
+        cast(nc.scalar.copy, second, 1, 1, 2, 0, 64)
+        cast(nc.vector.tensor_copy, second, 1, 1, 2, 64, P)
+        quantize_w(second, 1, 1, 2)
+        rest = sb("rest", [P, 2, P, PACK], BF16, tag="wb1")
+        cast(nc.vector.tensor_copy, rest, 1, 2, PACK, 0, P)
+        quantize_w(rest, 1, 2, PACK)
         h = [sb("h%d" % t, [P, S], F32) for t in range(PACK)]
         for t in range(PACK):
-            quantize_w(1, t, t + 1)
-            layer1(0, t)
+            if t == PACK - 1:
+                layer1(0, t)
             layer1(1, t)
             for hf in range(HALVES):
                 nc.scalar.activation(h[t][:, hf * BANK : (hf + 1) * BANK], acc[t][hf][:], GELU, bias=zero_bias[:])
@@ -160,7 +181,7 @@ def tile_picked_treeup_gelu_p_kernel(
         def turn_h(t, i):
             u, e = divmod(t, 2)
             if e == 0:
-                sums[u, i] = bank("sum%d_%d" % (u, i), 4 * u + i, [P, 2, 2, P])
+                sums[u, i] = bank("sum%d_%d" % (u, i), SUM_BANKS[u][i], [P, 2, 2, P])
             for n, b in enumerate(groups[i]):
                 nc.tensor.matmul(sums[u, i][:, n, e, :], h[t][:, b * P : (b + 1) * P], ident[:], start=(e == 0 and n == 0), stop=False, is_transpose=True)
 
@@ -184,7 +205,7 @@ def tile_picked_treeup_gelu_p_kernel(
 
         def turn_back(u, i):
             if u == 0:
-                backs[i] = bank("back%d" % i, i, [P, 2, 2, P])
+                backs[i] = bank("back%d" % i, SUM_BANKS[0][i], [P, 2, 2, P])
             for n in range(len(groups[i])):
                 nc.tensor.transpose(backs[i][:, n, u, :], rounded[u, i][:, n, :, :].rearrange("j p e -> j (p e)").bitcast(F32), ident[:])
 
@@ -252,4 +273,4 @@ def tile_picked_treeup_gelu_p_kernel(
         quantize_z(BANK, 768)
         layer2(BANK, 768, 5, nc.scalar.copy)
         quantize_z(768, S)
-        layer2(768, S, 6, nc.vector.tensor_copy)
+        layer2(768, S, 0, nc.vector.tensor_copy)

@@ -24,9 +24,7 @@ PASSES = K // (P * PACK)
 BANK = 512
 HALVES = S // BANK
 LAST = 384
-ROW0 = 12
 SUM_BANKS = ((6, 7, 2), (4, 5, 3))
-PLANE_START = (12, 0)
 
 
 def tile_picked_treeup_gelu_p_kernel(
@@ -52,29 +50,26 @@ def tile_picked_treeup_gelu_p_kernel(
         zero_in = sb("zero_in", [P, 1], F32)
         zero_bias = sb("zero_bias", [P, 1], F32, tag="late")
 
-        nc.gpsimd.memset(xs[32:64, :].bitcast(I32), 0)
-        nc.gpsimd.memset(xs[0:ROW0, :].bitcast(I32), 0)
-        nc.gpsimd.memset(xs[64:P, :].bitcast(I32), 0)
         make_identity(nc, ident[:])
         nc.vector.memset(zero_in[:], 0.0)
+        nc.vector.memset(xs[32:64, :].bitcast(I32), 0)
+        nc.vector.memset(xs[64:P, :].bitcast(I32), 0)
         nc.scalar.activation(zero_bias[:], zero_in[:], GELU)
 
-        nc.sync.dma_start(offs_sb[:], offs)
-        nc.sync.dma_start(par_sb[:], par)
-
-        def load_x(g, c0, c1):
-            nc.sync.dma_start(xw[g][:, c0:c1].bitcast(I32), x_words[g][:, c0:c1, :].rearrange("p n t -> p (n t)").bitcast(I32))
+        def load_x(g):
+            nc.sync.dma_start(xw[g][:].bitcast(I32), x_words[g].rearrange("p n t -> p (n t)").bitcast(I32))
 
         def load_w(g):
             nc.sync.dma_start(raw[g][:], w1[g * 512 : (g + 1) * 512, :].rearrange("(p j) c -> p j c", j=PACK))
 
         share_col = sb("share_col", [P, S // P], F32)
+        nc.sync.dma_start(xs[0:32, :].bitcast(I32), x_scales.rearrange("g q n -> (g q) n").bitcast(I32))
+        nc.sync.dma_start(offs_sb[:], offs)
         nc.sync.dma_start(share_col[:], share[0:1, :].rearrange("o (p c) -> (o p) c", p=P))
-        load_x(0, 0, T // 4)
-        nc.sync.dma_start(xs[ROW0 : ROW0 + 32, :].bitcast(I32), x_scales.rearrange("g q n -> (g q) n").bitcast(I32))
-        load_x(0, T // 4, T)
+        load_x(0)
+        nc.sync.dma_start(par_sb[:], par)
         load_w(0)
-        load_x(1, 0, T)
+        load_x(1)
 
         share_sb = sb("share_sb", [P, S], F32)
         for hf in range(HALVES):
@@ -88,17 +83,22 @@ def tile_picked_treeup_gelu_p_kernel(
 
         gw = [sb("gw%d" % g, [P, S], U32) for g in range(PASSES)]
         gs = sb("gs", [P, S], U8)
-        planes = sb("planes", [P, S], U8)
         nc.vector.tensor_copy(gs[:], xs[:].indirect(offs_sb[:]))
-        nc.vector.tensor_copy(planes[:].bitcast(I32), gs[:].bitcast(I32))
-        for g in range(PASSES):
-            for q in range(4):
-                source, target = ROW0 + 16 * g + 4 * q, 32 * q + PLANE_START[g]
-                if source != target:
-                    nc.scalar.dma_start(planes[target : target + 4, :].bitcast(I32), gs[source : source + 4, :].bitcast(I32))
+
+        def place_scales(queue, g, q):
+            queue.dma_start(planes[g][32 * q : 32 * q + 4, :].bitcast(I32), gs[16 * g + 4 * q : 16 * g + 4 * q + 4, :].bitcast(I32))
+
+        planes = [sb("plane0", [P, S], U8)]
+        nc.vector.tensor_copy(planes[0][:].bitcast(I32), gs[:].bitcast(I32))
+        for q in range(1, 4):
+            place_scales(nc.scalar, 0, q)
         raw.append(sb("raw1", [P, PACK, H], F32, tag="xs"))
         load_w(1)
         nc.vector.tensor_copy(gw[0][:], xw[0][:].indirect(offs_sb[:]))
+        planes.append(sb("plane1", [P, S], U8, tag="xw0"))
+        nc.gpsimd.memset(planes[1][:].bitcast(I32), 0)
+        for q in range(4):
+            place_scales(nc.sync, 1, q)
         wq = [sb("wq%d" % g, [P, H], U32) for g in range(PASSES)]
         wsc = [sb("wsc%d" % g, [P, H], U8) for g in range(PASSES)]
 
@@ -127,14 +127,14 @@ def tile_picked_treeup_gelu_p_kernel(
                     lhsT=wq[g][:, P * t : P * (t + 1)].bitcast(FP8X4),
                     lhsT_scale=wsc[g][:, P * t : P * (t + 1)],
                     rhs=gw[g][:, cols].bitcast(FP8X4),
-                    rhs_scale=planes[PLANE_START[g] : P, cols],
+                    rhs_scale=planes[g][:, cols],
                     start=(g == 0),
                     stop=(g == PASSES - 1),
                 )
 
         wb0 = sb("wb0", [P, PACK, P, PACK], BF16)
-        cast(nc.scalar.copy, wb0, 0, 0, PACK, 0, 80)
-        cast(nc.vector.tensor_copy, wb0, 0, 0, PACK, 80, P)
+        cast(nc.scalar.copy, wb0, 0, 0, PACK, 0, 88)
+        cast(nc.vector.tensor_copy, wb0, 0, 0, PACK, 88, P)
         quantize_w(wb0, 0, 0, PACK)
         for t in range(PACK - 1):
             layer1(0, t)
@@ -259,9 +259,9 @@ def tile_picked_treeup_gelu_p_kernel(
 
         def add(c0, c1):
             nc.vector.tensor_tensor(
-                zq_cols(c0, c1).rearrange("p (c i) t -> p c t i", i=4),
-                last[:, :, c0 - TURNED : c1 - TURNED].rearrange("p t (c i) -> p c t i", i=4),
-                h_last[:, :, c0 - TURNED : c1 - TURNED].rearrange("p t (c i) -> p c t i", i=4),
+                zq_cols(c0, c1).rearrange("p (c i) t -> p c t i", i=2),
+                last[:, :, c0 - TURNED : c1 - TURNED].rearrange("p t (c i) -> p c t i", i=2),
+                h_last[:, :, c0 - TURNED : c1 - TURNED].rearrange("p t (c i) -> p c t i", i=2),
                 ADD,
             )
 

@@ -24,6 +24,7 @@ PASSES = K // (P * PACK)
 BANK = 512
 HALVES = S // BANK
 LAST = 384
+ACC_BANKS = ((0, 1, 6, 7), (2, 3), (4, 5), (0, 1))
 SUM_BANKS = ((6, 7, 2), (4, 5, 3))
 
 
@@ -96,7 +97,7 @@ def tile_picked_treeup_gelu_p_kernel(
         load_w(1)
         nc.vector.tensor_copy(gw[0][:], xw[0][:].indirect(offs_sb[:]))
         planes.append(sb("plane1", [P, S], U8, tag="xw0"))
-        nc.gpsimd.memset(planes[1][:].bitcast(I32), 0)
+        nc.vector.memset(planes[1][:].bitcast(I32), 0)
         for q in range(4):
             place_scales(nc.sync, 1, q)
         wq = [sb("wq%d" % g, [P, H], U32) for g in range(PASSES)]
@@ -119,9 +120,10 @@ def tile_picked_treeup_gelu_p_kernel(
 
         def layer1(g, t):
             if g == 0:
-                acc[t] = [bank("acc%d_%d" % (t, hf), HALVES * (t % 3) + hf, [P, BANK]) for hf in range(HALVES)]
-            for hf in range(HALVES):
-                cols = slice(hf * BANK, (hf + 1) * BANK)
+                acc[t] = [bank("acc%d_%d" % (t, b), b, [P, S // len(ACC_BANKS[t])]) for b in ACC_BANKS[t]]
+            width = S // len(acc[t])
+            for hf in range(len(acc[t])):
+                cols = slice(hf * width, (hf + 1) * width)
                 nc.tensor.matmul_mx(
                     out=acc[t][hf][:],
                     lhsT=wq[g][:, P * t : P * (t + 1)].bitcast(FP8X4),
@@ -141,28 +143,28 @@ def tile_picked_treeup_gelu_p_kernel(
         w2w = sb("w2w", [P, 2 * N], U8, tag="wb0")
         nc.sync.dma_start(w2w[:].bitcast(I32), w2_words[0].bitcast(I32))
         nc.vector.tensor_copy(gw[1][:], xw[1][:].indirect(offs_sb[:]))
-        w2s = sb("w2s", [P, N], U8, tag="xw1")
-        nc.gpsimd.memset(w2s[:].bitcast(I32), 0)
-        for q in range(4):
-            nc.sync.dma_start(w2s[32 * q : 32 * q + 4, :].bitcast(I32), w2_scales[0, 4 * q : 4 * q + 4, :].bitcast(I32))
         first = sb("first", [P, 1, P, PACK], BF16, tag="wb1")
         cast(nc.scalar.copy, first, 1, 0, 1, 0, 48)
         cast(nc.vector.tensor_copy, first, 1, 0, 1, 48, P)
         quantize_w(first, 1, 0, 1)
         second = sb("second", [P, 1, P, PACK], BF16)
-        cast(nc.scalar.copy, second, 1, 1, 2, 0, 64)
-        cast(nc.vector.tensor_copy, second, 1, 1, 2, 64, P)
-        quantize_w(second, 1, 1, 2)
+        cast(nc.scalar.copy, second, 1, 1, 2, 0, P)
         rest = sb("rest", [P, 2, P, PACK], BF16, tag="wb1")
         cast(nc.vector.tensor_copy, rest, 1, 2, PACK, 0, P)
+        quantize_w(second, 1, 1, 2)
         quantize_w(rest, 1, 2, PACK)
+        w2s = sb("w2s", [P, N], U8, tag="wb1")
+        nc.vector.memset(w2s[:].bitcast(I32), 0)
+        for q in range(4):
+            nc.sync.dma_start(w2s[32 * q : 32 * q + 4, :].bitcast(I32), w2_scales[0, 4 * q : 4 * q + 4, :].bitcast(I32))
         h = [sb("h%d" % t, [P, S], F32) for t in range(PACK)]
         for t in range(PACK):
             if t == PACK - 1:
                 layer1(0, t)
             layer1(1, t)
-            for hf in range(HALVES):
-                nc.scalar.activation(h[t][:, hf * BANK : (hf + 1) * BANK], acc[t][hf][:], GELU, bias=zero_bias[:])
+            width = S // len(acc[t])
+            for hf in range(len(acc[t])):
+                nc.scalar.activation(h[t][:, hf * width : (hf + 1) * width], acc[t][hf][:], GELU, bias=zero_bias[:])
 
         TURNED = S - LAST
         groups = [list(range(b, min(b + 2, TURNED // P))) for b in range(0, TURNED // P, 2)]
@@ -259,9 +261,9 @@ def tile_picked_treeup_gelu_p_kernel(
 
         def add(c0, c1):
             nc.vector.tensor_tensor(
-                zq_cols(c0, c1).rearrange("p (c i) t -> p c t i", i=2),
-                last[:, :, c0 - TURNED : c1 - TURNED].rearrange("p t (c i) -> p c t i", i=2),
-                h_last[:, :, c0 - TURNED : c1 - TURNED].rearrange("p t (c i) -> p c t i", i=2),
+                zq_cols(c0, c1).rearrange("p (c i) t -> p c t i", i=4),
+                last[:, :, c0 - TURNED : c1 - TURNED].rearrange("p t (c i) -> p c t i", i=4),
+                h_last[:, :, c0 - TURNED : c1 - TURNED].rearrange("p t (c i) -> p c t i", i=4),
                 ADD,
             )
 

@@ -21,11 +21,18 @@ ADD = mybir.AluOpType.add
 P = 128
 PACK = 4
 PASSES = K // (P * PACK)
+QUADRANTS = 4
 BANK = 512
-HALVES = S // BANK
-LAST = 384
+LIST_ROWS = 16
+
+ADDED = 384
+TURNED = S - ADDED
+SCALAR_SHARE_PASS0 = 88
+SCALAR_SHARE_PASS1 = 52
 ACC_BANKS = ((0, 1, 6, 7), (2, 3), (4, 5), (0, 1))
+PLANES_AHEAD = 3
 SUM_BANKS = ((6, 7, 2), (4, 5, 3))
+PIECES = ((0, 512), (512, 768), (768, S))
 
 
 def tile_picked_treeup_gelu_p_kernel(
@@ -42,8 +49,8 @@ def tile_picked_treeup_gelu_p_kernel(
         def bank(name, b, shape):
             return psum.tile(shape, F32, name=name, tag="bank%d" % b)
 
-        offs_sb = sb("offs_sb", [P, S // 16], U16)
-        par_sb = sb("par_sb", [P, S // 16], U16)
+        offs_sb = sb("offs_sb", [P, S // LIST_ROWS], U16)
+        par_sb = sb("par_sb", [P, S // LIST_ROWS], U16)
         xw = [sb("xw%d" % g, [P, T], U32) for g in range(PASSES)]
         xs = sb("xs", [P, T], U8)
         raw = [sb("raw0", [P, PACK, H], F32)]
@@ -61,7 +68,7 @@ def tile_picked_treeup_gelu_p_kernel(
             nc.sync.dma_start(xw[g][:].bitcast(I32), x_words[g].rearrange("p n t -> p (n t)").bitcast(I32))
 
         def load_w(g):
-            nc.sync.dma_start(raw[g][:], w1[g * 512 : (g + 1) * 512, :].rearrange("(p j) c -> p j c", j=PACK))
+            nc.sync.dma_start(raw[g][:], w1[g * P * PACK : (g + 1) * P * PACK, :].rearrange("(p j) c -> p j c", j=PACK))
 
         share_col = sb("share_col", [P, S // P], F32)
         nc.sync.dma_start(xs[0:32, :].bitcast(I32), x_scales.rearrange("g q n -> (g q) n").bitcast(I32))
@@ -73,7 +80,7 @@ def tile_picked_treeup_gelu_p_kernel(
         load_x(1)
 
         share_sb = sb("share_sb", [P, S], F32)
-        for hf in range(HALVES):
+        for hf in range(S // BANK):
             spread = bank("spread%d" % hf, hf, [P, PACK, P])
             for c in range(PACK):
                 nc.tensor.transpose(spread[:, c, :], share_col[:, PACK * hf + c : PACK * hf + c + 1].to_broadcast([P, P]), ident[:])
@@ -87,93 +94,90 @@ def tile_picked_treeup_gelu_p_kernel(
         nc.vector.tensor_copy(gs[:], xs[:].indirect(offs_sb[:]))
 
         def place_scales(queue, g, q):
-            queue.dma_start(planes[g][32 * q : 32 * q + 4, :].bitcast(I32), gs[16 * g + 4 * q : 16 * g + 4 * q + 4, :].bitcast(I32))
+            queue.dma_start(x_scale[g][32 * q : 32 * q + 4, :].bitcast(I32), gs[16 * g + 4 * q : 16 * g + 4 * q + 4, :].bitcast(I32))
 
-        planes = [sb("plane0", [P, S], U8)]
-        nc.vector.tensor_copy(planes[0][:].bitcast(I32), gs[:].bitcast(I32))
-        for q in range(1, 4):
+        x_scale = [sb("plane0", [P, S], U8)]
+        nc.vector.tensor_copy(x_scale[0][:].bitcast(I32), gs[:].bitcast(I32))
+        for q in range(1, QUADRANTS):
             place_scales(nc.scalar, 0, q)
         raw.append(sb("raw1", [P, PACK, H], F32, tag="xs"))
         load_w(1)
         nc.vector.tensor_copy(gw[0][:], xw[0][:].indirect(offs_sb[:]))
-        planes.append(sb("plane1", [P, S], U8, tag="xw0"))
-        nc.vector.memset(planes[1][:].bitcast(I32), 0)
-        for q in range(4):
+        x_scale.append(sb("plane1", [P, S], U8, tag="xw0"))
+        nc.vector.memset(x_scale[1][:].bitcast(I32), 0)
+        for q in range(QUADRANTS):
             place_scales(nc.sync, 1, q)
         wq = [sb("wq%d" % g, [P, H], U32) for g in range(PASSES)]
         wsc = [sb("wsc%d" % g, [P, H], U8) for g in range(PASSES)]
 
         def cast(copy, wb, g, t0, t1, m0, m1):
             copy(
-                wb[:, :, m0:m1, :].rearrange("p t m j -> p m t j"),
-                raw[g][:, :, PACK * m0 : PACK * m1].rearrange("p j (m t) -> p m t j", t=PACK)[:, :, t0:t1, :],
+                wb[:, :, m0:m1, :].rearrange("p t m j -> p m j t"),
+                raw[g][:, :, PACK * m0 : PACK * m1].rearrange("p j (m t) -> p m j t", t=PACK)[:, :, :, t0:t1],
             )
 
         def quantize_w(wb, g, t0, t1):
             nc.vector.quantize_mx(
                 out=wq[g][:, P * t0 : P * t1].bitcast(FP8X4),
                 scales=wsc[g][:, P * t0 : P * t1],
-                in_=wb[:].rearrange("p t m j -> p (t m j)"),
+                in_=wb.rearrange("p t m j -> p (t m j)"),
             )
 
         acc = {}
 
         def layer1(g, t):
+            width = S // len(ACC_BANKS[t])
             if g == 0:
-                acc[t] = [bank("acc%d_%d" % (t, b), b, [P, S // len(ACC_BANKS[t])]) for b in ACC_BANKS[t]]
-            width = S // len(acc[t])
-            for hf in range(len(acc[t])):
-                cols = slice(hf * width, (hf + 1) * width)
+                acc[t] = [bank("acc%d_%d" % (t, b), b, [P, width]) for b in ACC_BANKS[t]]
+            for n, tile in enumerate(acc[t]):
+                cols = slice(n * width, (n + 1) * width)
                 nc.tensor.matmul_mx(
-                    out=acc[t][hf][:],
+                    out=tile[:],
                     lhsT=wq[g][:, P * t : P * (t + 1)].bitcast(FP8X4),
                     lhsT_scale=wsc[g][:, P * t : P * (t + 1)],
                     rhs=gw[g][:, cols].bitcast(FP8X4),
-                    rhs_scale=planes[g][:, cols],
+                    rhs_scale=x_scale[g][:, cols],
                     start=(g == 0),
                     stop=(g == PASSES - 1),
                 )
 
         wb0 = sb("wb0", [P, PACK, P, PACK], BF16)
-        cast(nc.scalar.copy, wb0, 0, 0, PACK, 0, 88)
-        cast(nc.vector.tensor_copy, wb0, 0, 0, PACK, 88, P)
-        quantize_w(wb0, 0, 0, PACK)
-        for t in range(PACK - 1):
+        cast(nc.scalar.copy, wb0, 0, 0, PACK, 0, SCALAR_SHARE_PASS0)
+        cast(nc.vector.tensor_copy, wb0, 0, 0, PACK, SCALAR_SHARE_PASS0, P)
+        quantize_w(wb0[:], 0, 0, PACK)
+        for t in range(PLANES_AHEAD):
             layer1(0, t)
         w2w = sb("w2w", [P, 2 * N], U8, tag="wb0")
         nc.sync.dma_start(w2w[:].bitcast(I32), w2_words[0].bitcast(I32))
         nc.vector.tensor_copy(gw[1][:], xw[1][:].indirect(offs_sb[:]))
-        first = sb("first", [P, 1, P, PACK], BF16, tag="wb1")
-        cast(nc.scalar.copy, first, 1, 0, 1, 0, 48)
-        cast(nc.vector.tensor_copy, first, 1, 0, 1, 48, P)
-        quantize_w(first, 1, 0, 1)
-        second = sb("second", [P, 1, P, PACK], BF16)
-        cast(nc.scalar.copy, second, 1, 1, 2, 0, P)
+        lower = sb("lower", [P, 2, P, PACK], BF16, tag="wb1")
+        cast(nc.scalar.copy, lower, 1, 0, 2, 0, SCALAR_SHARE_PASS1)
+        cast(nc.vector.tensor_copy, lower, 1, 0, 2, SCALAR_SHARE_PASS1, P)
+        for t in range(2):
+            quantize_w(lower[:, t : t + 1, :, :], 1, t, t + 1)
         rest = sb("rest", [P, 2, P, PACK], BF16, tag="wb1")
         cast(nc.vector.tensor_copy, rest, 1, 2, PACK, 0, P)
-        quantize_w(second, 1, 1, 2)
-        quantize_w(rest, 1, 2, PACK)
+        quantize_w(rest[:], 1, 2, PACK)
         w2s = sb("w2s", [P, N], U8, tag="wb1")
         nc.vector.memset(w2s[:].bitcast(I32), 0)
-        for q in range(4):
+        for q in range(QUADRANTS):
             nc.sync.dma_start(w2s[32 * q : 32 * q + 4, :].bitcast(I32), w2_scales[0, 4 * q : 4 * q + 4, :].bitcast(I32))
         h = [sb("h%d" % t, [P, S], F32) for t in range(PACK)]
         for t in range(PACK):
-            if t == PACK - 1:
+            if t >= PLANES_AHEAD:
                 layer1(0, t)
             layer1(1, t)
             width = S // len(acc[t])
-            for hf in range(len(acc[t])):
-                nc.scalar.activation(h[t][:, hf * width : (hf + 1) * width], acc[t][hf][:], GELU, bias=zero_bias[:])
+            for n, tile in enumerate(acc[t]):
+                nc.scalar.activation(h[t][:, n * width : (n + 1) * width], tile[:], GELU, bias=zero_bias[:])
 
-        TURNED = S - LAST
         groups = [list(range(b, min(b + 2, TURNED // P))) for b in range(0, TURNED // P, 2)]
-        h_last = sb("h_last", [P, PACK, LAST], F32)
+        h_last = sb("h_last", [P, PACK, ADDED], F32)
 
         taken = {}
 
         def follow(dst, t, c0, c1):
-            nc.vector.tensor_tensor(dst, h[t][:].indirect(par_sb[:, c0 // 16 : c1 // 16]), share_sb[:, c0:c1], MULT)
+            nc.vector.tensor_tensor(dst, h[t][:].indirect(par_sb[:, c0 // LIST_ROWS : c1 // LIST_ROWS]), share_sb[:, c0:c1], MULT)
             for b in range(c0 // P, c1 // P):
                 taken[t, b] = dst[:, b * P - c0 : (b + 1) * P - c0]
 
@@ -196,11 +200,10 @@ def tile_picked_treeup_gelu_p_kernel(
             nb = len(groups[i])
             nc.scalar.copy(rounded[u, i][:, 0:nb, :, :], sums[u, i][:, 0:nb, :, :].rearrange("j n e p -> j n p e"))
 
-        pieces = [(0, 512), (512, 768), (768, S)]
-        zq = {c0: sb("zq%d" % c0, [P, c1 - c0, PACK], BF16) for c0, c1 in pieces[:2]}
+        zq = {c0: sb("zq%d" % c0, [P, c1 - c0, PACK], BF16) for c0, c1 in PIECES[:2]}
 
         def zq_cols(c0, c1):
-            start = max(a for a, b in pieces if a <= c0)
+            start = max(a for a, b in PIECES if a <= c0)
             return zq[start][:, c0 - start : c1 - start, :]
 
         backs = {}
@@ -222,10 +225,9 @@ def tile_picked_treeup_gelu_p_kernel(
         zc = sb("zc", [P, S], U32)
         zs = sb("zs", [P, S], U8)
 
-        def quantize_z(c0, c1):
+        def layer2(piece, bk, copy):
+            c0, c1 = piece
             nc.vector.quantize_mx(out=zc[:, c0:c1].bitcast(FP8X4), scales=zs[:, c0:c1], in_=zq_cols(c0, c1).rearrange("p j t -> p (j t)"))
-
-        def layer2(c0, c1, bk, copy):
             y = bank("y%d" % c0, bk, [P, c1 - c0])
             nc.tensor.matmul_mx(out=y[:], lhsT=w2w[:].bitcast(FP4X4), lhsT_scale=w2s[:], rhs=zc[:, c0:c1].bitcast(FP8X4), rhs_scale=zs[:, c0:c1], start=True, stop=True)
             res = sb("res%d" % c0, [P, c1 - c0], F32)
@@ -255,7 +257,7 @@ def tile_picked_treeup_gelu_p_kernel(
             weave(i)
         for t in range(PACK):
             nc.sync.dma_start(h_last[:, t, :], h[t][:, TURNED:S])
-        last = sb("last", [P, PACK, LAST], F32, tag="late")
+        last = sb("last", [P, PACK, ADDED], F32, tag="late")
         for t in range(PACK):
             follow(last[:, t, :], t, TURNED, S)
 
@@ -267,12 +269,9 @@ def tile_picked_treeup_gelu_p_kernel(
                 ADD,
             )
 
-        quantize_z(0, BANK)
-        layer2(0, BANK, len(groups) - 1, nc.scalar.copy)
-        add(TURNED, 768)
-        zq[768] = sb("zq768", [P, 256, PACK], BF16, tag="zq0")
-        add(768, S)
-        quantize_z(BANK, 768)
-        layer2(BANK, 768, 5, nc.scalar.copy)
-        quantize_z(768, S)
-        layer2(768, S, 0, nc.vector.tensor_copy)
+        layer2(PIECES[0], SUM_BANKS[0][-1], nc.scalar.copy)
+        add(TURNED, PIECES[1][1])
+        zq[PIECES[2][0]] = sb("zq%d" % PIECES[2][0], [P, S - PIECES[2][0], PACK], BF16, tag="zq0")
+        add(*PIECES[2])
+        layer2(PIECES[1], SUM_BANKS[1][1], nc.scalar.copy)
+        layer2(PIECES[2], ACC_BANKS[PACK - 1][0], nc.vector.tensor_copy)

@@ -15,6 +15,7 @@ U8 = mybir.dt.uint8
 FP8X4 = mybir.dt.float8_e4m3fn_x4
 FP4X4 = mybir.dt.float4_e2m1fn_x4
 GELU = mybir.ActivationFunctionType.Gelu_apprx_tanh
+COPY = mybir.ActivationFunctionType.Copy
 MULT = mybir.AluOpType.mult
 ADD = mybir.AluOpType.add
 
@@ -27,6 +28,7 @@ LIST_ROWS = 16
 
 ADDED = 384
 TURNED = S - ADDED
+FETCHED = 3
 SCALAR_SHARE_PASS0 = 88
 SCALAR_SHARE_PASS1 = 52
 ACC_BANKS = ((0, 1, 6, 7), (2, 3), (4, 5), (0, 1))
@@ -200,7 +202,7 @@ def tile_picked_treeup_gelu_p_kernel(
             nb = len(groups[i])
             nc.scalar.copy(rounded[u, i][:, 0:nb, :, :], sums[u, i][:, 0:nb, :, :].rearrange("j n e p -> j n p e"))
 
-        zq = {c0: sb("zq%d" % c0, [P, c1 - c0, PACK], BF16) for c0, c1 in PIECES[:2]}
+        zq = {c0: sb("zq%d" % c0, [P, c1 - c0, PACK], BF16) for c0, c1 in PIECES}
 
         def zq_cols(c0, c1):
             start = max(a for a, b in PIECES if a <= c0)
@@ -234,6 +236,9 @@ def tile_picked_treeup_gelu_p_kernel(
             copy(res[:], y[:])
             nc.sync.dma_start(out[:, c0:c1], res[:])
 
+        last = sb("last", [P, PACK, ADDED], F32, tag="late")
+        for t in range(FETCHED):
+            nc.scalar.activation(last[:, t, :], h[t][:].indirect(par_sb[:, TURNED // LIST_ROWS :]), COPY)
         early = sb("early", [P, PACK, TURNED], F32)
         every = range(len(groups))
         for u in range(2):
@@ -251,15 +256,17 @@ def tile_picked_treeup_gelu_p_kernel(
                     follow(early[:, 3, c0:c1], 3, c0, c1)
                 turn_taken(2 * u + 1, i)
                 round_sums(u, i)
-            for i in every:
-                turn_back(u, i)
         for i in every:
+            turn_back(0, i)
+            turn_back(1, i)
             weave(i)
         for t in range(PACK):
             nc.sync.dma_start(h_last[:, t, :], h[t][:, TURNED:S])
-        last = sb("last", [P, PACK, ADDED], F32, tag="late")
-        for t in range(PACK):
+        for t in range(FETCHED, PACK):
             follow(last[:, t, :], t, TURNED, S)
+        nc.vector.tensor_tensor(
+            last[:, 0:FETCHED, :], last[:, 0:FETCHED, :], share_sb[:, TURNED:S].unsqueeze(1).to_broadcast([P, FETCHED, ADDED]), MULT
+        )
 
         def add(c0, c1):
             nc.vector.tensor_tensor(
@@ -269,9 +276,8 @@ def tile_picked_treeup_gelu_p_kernel(
                 ADD,
             )
 
-        layer2(PIECES[0], SUM_BANKS[0][-1], nc.scalar.copy)
-        add(TURNED, PIECES[1][1])
-        zq[PIECES[2][0]] = sb("zq%d" % PIECES[2][0], [P, S - PIECES[2][0], PACK], BF16, tag="zq0")
         add(*PIECES[2])
-        layer2(PIECES[1], SUM_BANKS[1][1], nc.scalar.copy)
-        layer2(PIECES[2], ACC_BANKS[PACK - 1][0], nc.vector.tensor_copy)
+        add(TURNED, PIECES[1][1])
+        layer2(PIECES[2], SUM_BANKS[0][-1], nc.vector.tensor_copy)
+        layer2(PIECES[0], SUM_BANKS[1][0], nc.scalar.copy)
+        layer2(PIECES[1], SUM_BANKS[1][1], nc.vector.tensor_copy)

@@ -34,7 +34,7 @@ SCALAR_SHARE_PASS1 = 52
 ACC_BANKS = ((0, 1, 6, 7), (2, 3), (4, 5), (0, 1))
 PLANES_AHEAD = 3
 SUM_BANKS = ((6, 7, 2), (4, 5, 3))
-PIECES = ((0, 512), (512, 768), (768, S))
+PIECES = ((0, 256), (256, 512), (512, 768), (768, S))
 
 
 def tile_picked_treeup_gelu_p_kernel(
@@ -264,20 +264,21 @@ def tile_picked_treeup_gelu_p_kernel(
             nc.sync.dma_start(h_last[:, t, :], h[t][:, TURNED:S])
         for t in range(FETCHED, PACK):
             follow(last[:, t, :], t, TURNED, S)
-        nc.vector.tensor_tensor(
-            last[:, 0:FETCHED, :], last[:, 0:FETCHED, :], share_sb[:, TURNED:S].unsqueeze(1).to_broadcast([P, FETCHED, ADDED]), MULT
-        )
+        for c0, c1 in (PIECES[3], (TURNED, PIECES[2][1])):
+            cols = last[:, 0:FETCHED, c0 - TURNED : c1 - TURNED]
+            nc.vector.tensor_tensor(cols, cols, share_sb[:, c0:c1].unsqueeze(1).to_broadcast([P, FETCHED, c1 - c0]), MULT)
 
         def add(c0, c1):
             nc.vector.tensor_tensor(
-                zq_cols(c0, c1).rearrange("p (c i) t -> p c t i", i=4),
-                last[:, :, c0 - TURNED : c1 - TURNED].rearrange("p t (c i) -> p c t i", i=4),
-                h_last[:, :, c0 - TURNED : c1 - TURNED].rearrange("p t (c i) -> p c t i", i=4),
+                zq_cols(c0, c1).rearrange("p (c i) t -> p c t i", i=2),
+                last[:, :, c0 - TURNED : c1 - TURNED].rearrange("p t (c i) -> p c t i", i=2),
+                h_last[:, :, c0 - TURNED : c1 - TURNED].rearrange("p t (c i) -> p c t i", i=2),
                 ADD,
             )
 
-        add(*PIECES[2])
-        add(TURNED, PIECES[1][1])
-        layer2(PIECES[2], SUM_BANKS[0][-1], nc.vector.tensor_copy)
+        add(*PIECES[3])
+        add(TURNED, PIECES[2][1])
+        layer2(PIECES[3], SUM_BANKS[0][-1], nc.scalar.copy)
         layer2(PIECES[0], SUM_BANKS[1][0], nc.scalar.copy)
-        layer2(PIECES[1], SUM_BANKS[1][1], nc.vector.tensor_copy)
+        layer2(PIECES[1], SUM_BANKS[1][1], nc.scalar.copy)
+        layer2(PIECES[2], SUM_BANKS[1][2], nc.vector.tensor_copy)

@@ -24,6 +24,8 @@ PACK = 4
 PASSES = K // (P * PACK)
 QUADRANTS = 4
 BANK = 512
+ROWS_AT = 96
+PLANE_AT = (12, 0)
 LIST_ROWS = 16
 
 ADDED = 384
@@ -31,9 +33,9 @@ TURNED = S - ADDED
 FETCHED = 3
 SCALAR_SHARE_PASS0 = 88
 SCALAR_SHARE_PASS1 = 52
-ACC_BANKS = ((0, 1, 6, 7), (2, 3), (4, 5), (0, 1))
-PLANES_AHEAD = 3
-SUM_BANKS = ((6, 7, 2), (4, 5, 3))
+ACC_BANKS = ((0, 1, 6, 7), (2, 3), (0, 1), (6, 7))
+PLANES_AHEAD = 2
+SUM_BANKS = ((4, 5, 2), (3, 0, 1))
 PIECES = ((0, 256), (256, 512), (512, 768), (768, S))
 
 
@@ -62,8 +64,9 @@ def tile_picked_treeup_gelu_p_kernel(
 
         make_identity(nc, ident[:])
         nc.vector.memset(zero_in[:], 0.0)
-        nc.vector.memset(xs[32:64, :].bitcast(I32), 0)
-        nc.vector.memset(xs[64:P, :].bitcast(I32), 0)
+        nc.vector.memset(xs[0:ROWS_AT, :].bitcast(I32), 0)
+        x_scale = [sb("plane0", [P, S], U8)]
+        nc.vector.memset(x_scale[0][0:ROWS_AT, :].bitcast(I32), 0)
         nc.scalar.activation(zero_bias[:], zero_in[:], GELU)
 
         def load_x(g):
@@ -73,7 +76,7 @@ def tile_picked_treeup_gelu_p_kernel(
             nc.sync.dma_start(raw[g][:], w1[g * P * PACK : (g + 1) * P * PACK, :].rearrange("(p j) c -> p j c", j=PACK))
 
         share_col = sb("share_col", [P, S // P], F32)
-        nc.sync.dma_start(xs[0:32, :].bitcast(I32), x_scales.rearrange("g q n -> (g q) n").bitcast(I32))
+        nc.sync.dma_start(xs[ROWS_AT:P, :].bitcast(I32), x_scales.rearrange("g q n -> (g q) n").bitcast(I32))
         nc.sync.dma_start(offs_sb[:], offs)
         nc.sync.dma_start(share_col[:], share[0:1, :].rearrange("o (p c) -> (o p) c", p=P))
         load_x(0)
@@ -96,12 +99,12 @@ def tile_picked_treeup_gelu_p_kernel(
         nc.vector.tensor_copy(gs[:], xs[:].indirect(offs_sb[:]))
 
         def place_scales(queue, g, q):
-            queue.dma_start(x_scale[g][32 * q : 32 * q + 4, :].bitcast(I32), gs[16 * g + 4 * q : 16 * g + 4 * q + 4, :].bitcast(I32))
+            to, row = 32 * q + PLANE_AT[g], ROWS_AT + 16 * g + 4 * q
+            queue.dma_start(x_scale[g][to : to + 4, :].bitcast(I32), gs[row : row + 4, :].bitcast(I32))
 
-        x_scale = [sb("plane0", [P, S], U8)]
-        nc.vector.tensor_copy(x_scale[0][:].bitcast(I32), gs[:].bitcast(I32))
-        for q in range(1, QUADRANTS):
+        for q in range(QUADRANTS - 1):
             place_scales(nc.scalar, 0, q)
+        nc.vector.tensor_copy(x_scale[0][ROWS_AT:P, :].bitcast(I32), gs[ROWS_AT:P, :].bitcast(I32))
         raw.append(sb("raw1", [P, PACK, H], F32, tag="xs"))
         load_w(1)
         nc.vector.tensor_copy(gw[0][:], xw[0][:].indirect(offs_sb[:]))
@@ -138,7 +141,7 @@ def tile_picked_treeup_gelu_p_kernel(
                     lhsT=wq[g][:, P * t : P * (t + 1)].bitcast(FP8X4),
                     lhsT_scale=wsc[g][:, P * t : P * (t + 1)],
                     rhs=gw[g][:, cols].bitcast(FP8X4),
-                    rhs_scale=x_scale[g][:, cols],
+                    rhs_scale=x_scale[g][PLANE_AT[g] : P, cols],
                     start=(g == 0),
                     stop=(g == PASSES - 1),
                 )

from contextlib import ExitStack

import concourse.mybir as mybir
from concourse.masks import make_identity

K, T, S, H, N = 1024, 2048, 1024, 512, 128
FLOPS = 2 * K * H * S + 2 * H * N * S

F32 = mybir.dt.float32
BF16 = mybir.dt.bfloat16
I32 = mybir.dt.int32
U32 = mybir.dt.uint32
U16 = mybir.dt.uint16
U8 = mybir.dt.uint8
FP8X4 = mybir.dt.float8_e4m3fn_x4
FP4X4 = mybir.dt.float4_e2m1fn_x4
GELU = mybir.ActivationFunctionType.Gelu_apprx_tanh
COPY = mybir.ActivationFunctionType.Copy
MULT = mybir.AluOpType.mult
ADD = mybir.AluOpType.add

P = 128
PACK = 4
PASSES = K // (P * PACK)
QUADRANTS = 4
BANK = 512
ROWS_AT = 96
PLANE_AT = (12, 0)
LIST_ROWS = 16

ADDED = 384
TURNED = S - ADDED
FETCHED = 3
SCALAR_SHARE_PASS0 = 88
SCALAR_SHARE_PASS1 = 52
ACC_BANKS = ((0, 1, 6, 7), (2, 3), (0, 1), (6, 7))
PLANES_AHEAD = 2
SUM_BANKS = ((4, 5, 2), (3, 0, 1))
PIECES = ((0, 256), (256, 512), (512, 768), (768, S))


def tile_picked_treeup_gelu_p_kernel(
    tc, x_words, x_scales, w1, w2_words, w2_scales, share, offs, par, out
):
    nc = tc.nc
    with ExitStack() as ctx:
        keep = ctx.enter_context(tc.tile_pool(name="keep", bufs=1))
        psum = ctx.enter_context(tc.psum_pool(name="psum", bufs=1))

        def sb(name, shape, dtype, tag=None):
            return keep.tile(shape, dtype, name=name, tag=tag or name, align_bytes=64)

        def bank(name, b, shape):
            return psum.tile(shape, F32, name=name, tag="bank%d" % b)

        offs_sb = sb("offs_sb", [P, S // LIST_ROWS], U16)
        par_sb = sb("par_sb", [P, S // LIST_ROWS], U16)
        xw = [sb("xw%d" % g, [P, T], U32) for g in range(PASSES)]
        xs = sb("xs", [P, T], U8)
        raw = [sb("raw0", [P, PACK, H], F32)]
        ident = sb("ident", [P, P], F32)
        zero_in = sb("zero_in", [P, 1], F32)
        zero_bias = sb("zero_bias", [P, 1], F32, tag="late")

        make_identity(nc, ident[:])
        nc.vector.memset(zero_in[:], 0.0)
        nc.vector.memset(xs[0:ROWS_AT, :].bitcast(I32), 0)
        x_scale = [sb("plane0", [P, S], U8)]
        nc.vector.memset(x_scale[0][0:ROWS_AT, :].bitcast(I32), 0)
        nc.scalar.activation(zero_bias[:], zero_in[:], GELU)

        def load_x(g):
            nc.sync.dma_start(xw[g][:].bitcast(I32), x_words[g].rearrange("p n t -> p (n t)").bitcast(I32))

        def load_w(g):
            nc.sync.dma_start(raw[g][:], w1[g * P * PACK : (g + 1) * P * PACK, :].rearrange("(p j) c -> p j c", j=PACK))

        share_col = sb("share_col", [P, S // P], F32)
        nc.sync.dma_start(xs[ROWS_AT:P, :].bitcast(I32), x_scales.rearrange("g q n -> (g q) n").bitcast(I32))
        nc.sync.dma_start(offs_sb[:], offs)
        nc.sync.dma_start(share_col[:], share[0:1, :].rearrange("o (p c) -> (o p) c", p=P))
        load_x(0)
        nc.sync.dma_start(par_sb[:], par)
        load_w(0)
        load_x(1)

        share_sb = sb("share_sb", [P, S], F32)
        for hf in range(S // BANK):
            spread = bank("spread%d" % hf, hf, [P, PACK, P])
            for c in range(PACK):
                nc.tensor.transpose(spread[:, c, :], share_col[:, PACK * hf + c : PACK * hf + c + 1].to_broadcast([P, P]), ident[:])
            nc.scalar.copy(
                share_sb[:].rearrange("p (j c) -> p j c", c=S // P)[:, :, PACK * hf : PACK * (hf + 1)],
                spread[:].rearrange("p c j -> p j c"),
            )

        gw = [sb("gw%d" % g, [P, S], U32) for g in range(PASSES)]
        gs = sb("gs", [P, S], U8)
        nc.vector.tensor_copy(gs[:], xs[:].indirect(offs_sb[:]))

        def place_scales(queue, g, q):
            to, row = 32 * q + PLANE_AT[g], ROWS_AT + 16 * g + 4 * q
            queue.dma_start(x_scale[g][to : to + 4, :].bitcast(I32), gs[row : row + 4, :].bitcast(I32))

        for q in range(QUADRANTS - 1):
            place_scales(nc.scalar, 0, q)
        nc.vector.tensor_copy(x_scale[0][ROWS_AT:P, :].bitcast(I32), gs[ROWS_AT:P, :].bitcast(I32))
        raw.append(sb("raw1", [P, PACK, H], F32, tag="xs"))
        load_w(1)
        nc.vector.tensor_copy(gw[0][:], xw[0][:].indirect(offs_sb[:]))
        x_scale.append(sb("plane1", [P, S], U8, tag="xw0"))
        nc.vector.memset(x_scale[1][:].bitcast(I32), 0)
        for q in range(QUADRANTS):
            place_scales(nc.sync, 1, q)
        wq = [sb("wq%d" % g, [P, H], U32) for g in range(PASSES)]
        wsc = [sb("wsc%d" % g, [P, H], U8) for g in range(PASSES)]

        def cast(copy, wb, g, t0, t1, m0, m1):
            copy(
                wb[:, :, m0:m1, :].rearrange("p t m j -> p m j t"),
                raw[g][:, :, PACK * m0 : PACK * m1].rearrange("p j (m t) -> p m j t", t=PACK)[:, :, :, t0:t1],
            )

        def quantize_w(wb, g, t0, t1):
            nc.vector.quantize_mx(
                out=wq[g][:, P * t0 : P * t1].bitcast(FP8X4),
                scales=wsc[g][:, P * t0 : P * t1],
                in_=wb.rearrange("p t m j -> p (t m j)"),
            )

        acc = {}

        def layer1(g, t):
            width = S // len(ACC_BANKS[t])
            if g == 0:
                acc[t] = [bank("acc%d_%d" % (t, b), b, [P, width]) for b in ACC_BANKS[t]]
            for n, tile in enumerate(acc[t]):
                cols = slice(n * width, (n + 1) * width)
                nc.tensor.matmul_mx(
                    out=tile[:],
                    lhsT=wq[g][:, P * t : P * (t + 1)].bitcast(FP8X4),
                    lhsT_scale=wsc[g][:, P * t : P * (t + 1)],
                    rhs=gw[g][:, cols].bitcast(FP8X4),
                    rhs_scale=x_scale[g][PLANE_AT[g] : P, cols],
                    start=(g == 0),
                    stop=(g == PASSES - 1),
                )

        wb0 = sb("wb0", [P, PACK, P, PACK], BF16)
        cast(nc.scalar.copy, wb0, 0, 0, PACK, 0, SCALAR_SHARE_PASS0)
        cast(nc.vector.tensor_copy, wb0, 0, 0, PACK, SCALAR_SHARE_PASS0, P)
        quantize_w(wb0[:], 0, 0, PACK)
        for t in range(PLANES_AHEAD):
            layer1(0, t)
        w2w = sb("w2w", [P, 2 * N], U8, tag="wb0")
        nc.sync.dma_start(w2w[:].bitcast(I32), w2_words[0].bitcast(I32))
        nc.vector.tensor_copy(gw[1][:], xw[1][:].indirect(offs_sb[:]))
        lower = sb("lower", [P, 2, P, PACK], BF16, tag="wb1")
        cast(nc.scalar.copy, lower, 1, 0, 2, 0, SCALAR_SHARE_PASS1)
        cast(nc.vector.tensor_copy, lower, 1, 0, 2, SCALAR_SHARE_PASS1, P)
        for t in range(2):
            quantize_w(lower[:, t : t + 1, :, :], 1, t, t + 1)
        rest = sb("rest", [P, 2, P, PACK], BF16, tag="wb1")
        cast(nc.vector.tensor_copy, rest, 1, 2, PACK, 0, P)
        quantize_w(rest[:], 1, 2, PACK)
        w2s = sb("w2s", [P, N], U8, tag="wb1")
        nc.vector.memset(w2s[:].bitcast(I32), 0)
        for q in range(QUADRANTS):
            nc.sync.dma_start(w2s[32 * q : 32 * q + 4, :].bitcast(I32), w2_scales[0, 4 * q : 4 * q + 4, :].bitcast(I32))
        h = [sb("h%d" % t, [P, S], F32) for t in range(PACK)]
        for t in range(PACK):
            if t >= PLANES_AHEAD:
                layer1(0, t)
            layer1(1, t)
            width = S // len(acc[t])
            for n, tile in enumerate(acc[t]):
                nc.scalar.activation(h[t][:, n * width : (n + 1) * width], tile[:], GELU, bias=zero_bias[:])

        groups = [list(range(b, min(b + 2, TURNED // P))) for b in range(0, TURNED // P, 2)]
        h_last = sb("h_last", [P, PACK, ADDED], F32)

        taken = {}

        def follow(dst, t, c0, c1):
            nc.vector.tensor_tensor(dst, h[t][:].indirect(par_sb[:, c0 // LIST_ROWS : c1 // LIST_ROWS]), share_sb[:, c0:c1], MULT)
            for b in range(c0 // P, c1 // P):
                taken[t, b] = dst[:, b * P - c0 : (b + 1) * P - c0]

        sums = {}
        rounded = {(u, i): sb("rounded%d_%d" % (u, i), [P, 2, P, 2], BF16) for u in range(2) for i in range(len(groups))}

        def turn_h(t, i):
            u, e = divmod(t, 2)
            if e == 0:
                sums[u, i] = bank("sum%d_%d" % (u, i), SUM_BANKS[u][i], [P, 2, 2, P])
            for n, b in enumerate(groups[i]):
                nc.tensor.matmul(sums[u, i][:, n, e, :], h[t][:, b * P : (b + 1) * P], ident[:], start=(e == 0 and n == 0), stop=False, is_transpose=True)

        def turn_taken(t, i):
            u, e = divmod(t, 2)
            for n, b in enumerate(groups[i]):
                nc.tensor.matmul(sums[u, i][:, n, e, :], taken[t, b], ident[:], start=False, stop=(e == 1 and b == groups[i][-1]), is_transpose=True)

        def round_sums(u, i):
            nb = len(groups[i])
            nc.scalar.copy(rounded[u, i][:, 0:nb, :, :], sums[u, i][:, 0:nb, :, :].rearrange("j n e p -> j n p e"))

        zq = {c0: sb("zq%d" % c0, [P, c1 - c0, PACK], BF16) for c0, c1 in PIECES}

        def zq_cols(c0, c1):
            start = max(a for a, b in PIECES if a <= c0)
            return zq[start][:, c0 - start : c1 - start, :]

        backs = {}

        def turn_back(u, i):
            if u == 0:
                backs[i] = bank("back%d" % i, SUM_BANKS[0][i], [P, 2, 2, P])
            for n in range(len(groups[i])):
                nc.tensor.transpose(backs[i][:, n, u, :], rounded[u, i][:, n, :, :].rearrange("j p e -> j (p e)").bitcast(F32), ident[:])

        def weave(i):
            nb = len(groups[i])
            c0 = groups[i][0] * P
            nc.scalar.copy(
                zq_cols(c0, c0 + nb * P).rearrange("p j t -> p (j t)").bitcast(F32).rearrange("p (n j u) -> p n j u", n=nb, u=2),
                backs[i][:, 0:nb, :, :].rearrange("p n u j -> p n j u"),
            )

        zc = sb("zc", [P, S], U32)
        zs = sb("zs", [P, S], U8)

        def layer2(piece, bk, copy):
            c0, c1 = piece
            nc.vector.quantize_mx(out=zc[:, c0:c1].bitcast(FP8X4), scales=zs[:, c0:c1], in_=zq_cols(c0, c1).rearrange("p j t -> p (j t)"))
            y = bank("y%d" % c0, bk, [P, c1 - c0])
            nc.tensor.matmul_mx(out=y[:], lhsT=w2w[:].bitcast(FP4X4), lhsT_scale=w2s[:], rhs=zc[:, c0:c1].bitcast(FP8X4), rhs_scale=zs[:, c0:c1], start=True, stop=True)
            res = sb("res%d" % c0, [P, c1 - c0], F32)
            copy(res[:], y[:])
            nc.sync.dma_start(out[:, c0:c1], res[:])

        last = sb("last", [P, PACK, ADDED], F32, tag="late")
        for t in range(FETCHED):
            nc.scalar.activation(last[:, t, :], h[t][:].indirect(par_sb[:, TURNED // LIST_ROWS :]), COPY)
        early = sb("early", [P, PACK, TURNED], F32)
        every = range(len(groups))
        for u in range(2):
            for t in (2 * u, 2 * u + 1):
                for i in every:
                    turn_h(t, i)
            follow(early[:, 2 * u, :], 2 * u, 0, TURNED)
            for i in every:
                turn_taken(2 * u, i)
            if u == 0:
                follow(early[:, 1, :], 1, 0, TURNED)
            for i in every:
                c0, c1 = groups[i][0] * P, (groups[i][-1] + 1) * P
                if u == 1:
                    follow(early[:, 3, c0:c1], 3, c0, c1)
                turn_taken(2 * u + 1, i)
                round_sums(u, i)
        for i in every:
            turn_back(0, i)
            turn_back(1, i)
            weave(i)
        for t in range(PACK):
            nc.sync.dma_start(h_last[:, t, :], h[t][:, TURNED:S])
        for t in range(FETCHED, PACK):
            follow(last[:, t, :], t, TURNED, S)
        for c0, c1 in (PIECES[3], (TURNED, PIECES[2][1])):
            cols = last[:, 0:FETCHED, c0 - TURNED : c1 - TURNED]
            nc.vector.tensor_tensor(cols, cols, share_sb[:, c0:c1].unsqueeze(1).to_broadcast([P, FETCHED, c1 - c0]), MULT)

        def add(c0, c1):
            nc.vector.tensor_tensor(
                zq_cols(c0, c1).rearrange("p (c i) t -> p c t i", i=2),
                last[:, :, c0 - TURNED : c1 - TURNED].rearrange("p t (c i) -> p c t i", i=2),
                h_last[:, :, c0 - TURNED : c1 - TURNED].rearrange("p t (c i) -> p c t i", i=2),
                ADD,
            )

        add(*PIECES[3])
        add(TURNED, PIECES[2][1])
        layer2(PIECES[3], SUM_BANKS[0][-1], nc.scalar.copy)
        layer2(PIECES[0], SUM_BANKS[1][0], nc.scalar.copy)
        layer2(PIECES[1], SUM_BANKS[1][1], nc.scalar.copy)
        layer2(PIECES[2], SUM_BANKS[1][2], nc.vector.tensor_copy)
